import numpy as np, ml_dtypes
CORES = [6,15,38,47]
N = 4
import mx_ref
BF = ml_dtypes.bfloat16
def gentries(a):
    return np.ascontiguousarray(a.reshape(8, 16, -1).transpose(0, 2, 1)).reshape(8, -1)
def gtable(e):
    e = np.asarray(e); return np.ascontiguousarray(e.reshape(8, -1, 16).transpose(0, 2, 1)).reshape(128, -1).astype(np.int32)
def gcols(t, e):
    v = np.concatenate([t.reshape(8, 16, -1, 4), np.zeros((8, 16, 1, 4), BF)], axis=2)
    return np.ascontiguousarray(np.stack([v[g][:, e[g]] for g in range(8)])).reshape(128, -1)
def tile(rs):
    return np.stack(rs, axis=2).reshape(128, -1).astype(BF)
def pick(q, e):
    c = np.concatenate([q[0].reshape(128, -1, 4), np.zeros((128, 1, 4), np.uint8)], axis=1); s = np.concatenate([q[1], np.ones((16, 1), np.uint8)], axis=1)
    return (np.ascontiguousarray(c[:, e].reshape(128, -1)), np.ascontiguousarray(s[:, e]))
def join(*qs):
    return (np.concatenate([q[0] for q in qs], axis=1), np.concatenate([q[1] for q in qs], axis=1))
def put(q, e, v):
    c, s = q[0].reshape(128, -1, 4).copy(), q[1].copy(); c[:, e] = v[0].reshape(128, -1, 4); s[:, e] = v[1]
    return (c.reshape(128, -1), s)
def pk(c, s):
    return (np.ascontiguousarray(c), mx_ref.live(s))
def emit(q):
    return q[0], q[1]
def packed(v, rng):
    q = [mx_ref.quantize(np.ascontiguousarray(v[r])) for r in range(N)]
    return np.stack([a for a, b in q]), np.stack([mx_ref.plane(b, rng) for a, b in q])
def values_of_codes():
    e, c = np.zeros((128, 128, 4), np.float32), np.zeros((128, 2, 4), np.uint8)
    e[np.arange(128), np.arange(128), 0] = 1
    c[:127, :, 0] = np.arange(256).reshape(2, 128).T[:127]
    return mx_ref.matmul(mx_ref.quantize(e.reshape(128, 512).astype(BF)), (c.reshape(128, 8), np.full((16, 2), 127, np.uint8))).T.reshape(-1).astype(np.float64)
CODE_VALUE, SCALE_VALUE = values_of_codes(), 2.0 ** (np.arange(256) - 127.0)
def decode(q):
    return (CODE_VALUE[q[0]].reshape(16, 8, -1, 4) * SCALE_VALUE[q[1]][:, None, :, None] + 0.0).reshape(128, -1).astype(np.float32)
def f(rng, *shape):
    return mx_ref.flush((rng.standard_normal(shape, dtype=np.float32) * np.exp2(rng.integers(-2, 3, shape[:-1] + (1,)))).astype(BF))
def wide(rng, *shape, cols=0):
    v = rng.standard_normal(shape, dtype=np.float32) * np.exp2(rng.integers(-12, 13, shape)).astype(np.float32)
    if cols: v *= np.repeat(np.exp2(rng.integers(-cols, cols + 1, shape[:-2] + (1, shape[-1] // 4))) * (rng.random(shape[:-2] + (1, shape[-1] // 4)) > 0.0625), 4, axis=-1).astype(np.float32)
    return mx_ref.flush(v.astype(BF))
C, E, R = 192, 64, 3
def parts(m):
    return np.repeat(np.repeat(m, 16, axis=0), 4, axis=1)
def big(v):
    v = v.astype(np.float32)
    v[np.abs(v) < np.float32(2.0 ** -16)] = 0
    return v.astype(BF)
def numbers_of(rng):
    return {"x": big(f(rng, N, 128, 4 * C)), "u": np.array(f(rng, N, 128, 512)), "v": np.array(f(rng, N, 128, 512))}
def layer(rng, still=0):
    w = big(f(rng, N, 128, 2048)).reshape(N, 8, 16, 4, 8, 16, 4)
    w[:, :, :, :, :, :still] = 0
    return w
def moved(rng, rows):
    w = np.zeros((N, 128, 4, 128, 4), np.float32)
    for r in range(N):
        h, e = 16 * rng.integers(8), rng.integers(4)
        for b in range(4): w[r, (rows + h) % 128, b, rows, (b + e) % 4] = rng.choice([-16.0, 16.0], len(rows))
    return w.astype(BF)
def weights(rng, w, m):
    wc, ws = packed(np.ascontiguousarray(w).reshape(N, 128, 2048), rng)
    mc, ms = packed(np.ascontiguousarray(m).reshape(N, 128, 2048), rng)
    return {"wc": wc, "ws": ws, "mc": mc, "ms": ms}
def orders(rng):
    return np.argsort(rng.random((N, 8, 2 * R, C)), axis=3)
def lists(e):
    return np.stack([gtable(e[r].reshape(8, -1)) for r in range(N)])
def signs(rng):
    return np.stack([rng.permutation(8) % 2 * 2.0 - 1.0 for r in range(N)])
def setup_inputs(rng):
    return {**numbers_of(rng), **weights(rng, layer(rng), layer(rng)), "pl": lists(orders(rng))}
def setup_inputs_ties(rng):
    d = numbers_of(rng)
    e = rng.permutation(N)
    x = d["x"].reshape(N, 8, 16, C, 4)
    for r in range(N):
        k = np.zeros(C, int) if r == e[0] else rng.permutation(C) % 3
        a = x[r][:, :8, :3].copy()
        a[:, :, 2] = 0
        x[r][:, :8] = a[:, :, k]
    x[e[1], :, :8] = 0
    u = d["u"].reshape(N, 8, 16, 128, 4)
    for k in range(3): u[:, :, 8:, k::16] = 0
    return {"x": x.reshape(N, 128, 4 * C), "u": u.reshape(N, 128, 512), "v": d["v"], **weights(rng, layer(rng, 8), layer(rng, 8)), "pl": lists(orders(rng))}
def setup_inputs_near(rng):
    d = numbers_of(rng)
    x = np.zeros((N, 8, 16, C, 4), np.float32)
    u = d["u"].reshape(N, 128, 128, 4)
    for k in range(3): u[:, :, k::16] = 0
    o = rng.permutation(N) % 4
    c = [signs(rng), signs(rng)]
    j = np.arange(C)
    for r in range(N):
        size, one = (1.0, 1.0) if o[r] < 2 else (2.0 ** -4, 2.0 ** -27)
        for k in range(2):
            a = np.where(rng.permutation(8) % 2 == 0, E - 1, rng.integers(0, E, 8))[:, None]
            s = ((j + a) % E + rng.integers(0, 2, (8, 1))) // 2
            s[:, E:] = E // 2 + 1
            g = ((s[:, :, None] >> np.arange(8)) & 1) * np.exp2(np.arange(8) - 23.0) * size
            top = E - 1 - rng.integers(0, E // 8, (8, 1))
            if o[r] == 3:
                high = (j == top) | (j == 0) | (j >= E)
                x[r, :, k, :, 0] = (8 + high) * 2.0 ** -30
                x[r, :, 4 + k, :, 0] = (9 - high) * 2.0 ** -30
            else:
                if o[r] < 2: x[r, :, k, :, 0] = c[k][r][:, None]
                x[r, :, 8 + 2 * k] = g[:, :, :4]
                x[r, :, 9 + 2 * k] = g[:, :, 4:]
        x[r, :, 2, :, 0] = rng.integers(-1, 2, (8, C)) * one
        if o[r] == 2:
            x[r, :, 3] = x[r, :, 2]
            x[r, :, 2] *= 1.125
        if o[r] == 3:
            for g in rng.permutation(8)[:4]: x[r, g, 2, :, 0] = one
        x[r, :, 12:] = rng.integers(4, 8, (8, 4, C, 4)) * rng.choice([-1.0, 1.0], (8, 4, C, 4)) * 2.0 ** -20
        z = 1.0 if o[r] == 0 else 2.0 ** -30
        for h in range(0, 128, 16):
            for k in range(3): u[r, h + k, h + k, 0] = z
            for k in range(2): u[r, h + 8 + 2 * k:h + 10 + 2 * k, h + k] = z
            if o[r] == 2: u[r, h + 3, h + 2, 0] = -z
            if o[r] == 3:
                for k in range(2):
                    u[r, h + k, h + k, 0] = 1.125 * z
                    u[r, h + 4 + k, h + k, 0] = z
    rows = np.flatnonzero(np.arange(128) % 16 >= 12)
    return {"x": x.reshape(N, 128, 4 * C).astype(BF), "u": u.reshape(N, 128, 512), "v": d["v"], **weights(rng, moved(rng, rows), moved(rng, rows)), "pl": lists(orders(rng))}
def setup_inputs_huge(rng):
    d = numbers_of(rng)
    c = np.ones((N, C))
    for r in rng.permutation(N)[:N // 2]: c[r] = rng.permutation(C) % 2 * 2.0 - 1.0
    x = 2.0 ** 30 * (0.8 + 0.2 * rng.random((N, 128, C, 4))) * c[:, None, :, None]
    u = d["u"].reshape(N, 128, 8, 16, 4)
    a = 2.0 ** 30 * (1 - 0.1 * rng.random((N, 128, 8, 3, 4))) * np.stack([signs(rng), signs(rng), signs(rng)], axis=2)[:, None, :, :, None]
    u[:, :, :, :3] = a.astype(np.float32).astype(BF)
    rows = np.arange(128)
    return {"x": x.astype(np.float32).reshape(N, 128, 4 * C).astype(BF), "u": u.reshape(N, 128, 512), "v": d["v"], **weights(rng, moved(rng, rows), moved(rng, rows)), "pl": lists(orders(rng))}
def setup_inputs_places(rng):
    d = numbers_of(rng)
    x = d["x"].reshape(N, 8, 16, C, 4)
    x[:, :, :8] = 0
    u = d["u"].reshape(N, 128, 128, 4)
    for k in range(3): u[:, :, k::16] = 0
    for h in range(0, 128, 16):
        for k in range(3): u[:, h + k, h + k, 0] = 1
    e = orders(rng)
    for r in range(N):
        b = [rng.permutation(np.array([1, 2, E // 2 - 1, E // 2, E // 2 + 1, E - 1, rng.integers(1, E), rng.integers(1, E)])) for k in range(2)]
        same, kinds = rng.permutation(8)[:4], rng.permutation(8)
        b[1][same] = b[0][same]
        for g in range(8):
            for k in range(2):
                s = rng.integers(8, 16, C) * 0.0625
                s[0], s[E:], s[b[k][g]] = 4, 4, 2
                x[r, g, k, :, 0] = s
            s = rng.integers(-1, 2, C)
            if kinds[g] < 3: s[:] = kinds[g] - 1
            if kinds[g] == 3: s = (np.arange(C) == rng.integers(C)) * 2 - 1
            x[r, g, 2, :, 0] = s
        for i in range(2 * R):
            h = (r + i) % 4
            if h == 0: e[r, :, i] = np.arange(C)
            if h == 1: e[r, :, i] = np.arange(C)[::-1]
            if h == 2: e[r, :, i] = e[r, 0, i].copy()
    return {"x": x.reshape(N, 128, 4 * C), "u": u.reshape(N, 128, 512), "v": d["v"], **weights(rng, layer(rng, 8), layer(rng, 8)), "pl": lists(e)}
def setup_inputs_spread(rng):
    d = setup_inputs(rng)
    d["x"] = big(wide(rng, N, 128, 4 * C, cols=6))
    return d
def check_inputs(d):
    b = []
    for k in ("x", "u", "v"):
        a = np.abs(d[k].astype(np.float32))
        if not (np.isfinite(a).all() and ((a == 0) | (a >= 2.0 ** -30) & (a <= 2.0 ** 30)).all()): b.append("a value of " + k)
    none, least, most = [emit(mx_ref.quantize(np.full((128, 16), k, np.float32).astype(BF)))[1][0, 0] for k in (0.0, 2.0 ** -30, 2.0 ** 30)]
    for c, s in (("wc", "ws"), ("mc", "ms")):
        if ((d[c] & 0x7F) == 0x7F).any(): b.append("a code of " + c + " that is no number")
        for r in range(N):
            a = mx_ref.live(d[s][r])
            if ((a != none) & ((a < least) | (a > most))).any(): b.append("a scale of " + s)
    for r in range(N):
        e = gentries(d["pl"][r]).reshape(8, 2 * R, C)
        if not (np.sort(e, axis=2) == np.arange(C)).all(): b.append("a list of pl that is no permutation")
    return b
def reference(x, u, v, wc, ws, mc, ms, pl):
    qu = [mx_ref.quantize(u[r]) for r in range(N)]
    lay = [[pk(wc[r], ws[r]), pk(mc[r], ms[r])] for r in range(N)]
    at = [gentries(pl[r]).reshape(8, 2 * R, C) for r in range(N)]
    now = [x[r] for r in range(N)]
    place = np.arange(C)
    od = np.zeros((N, 8, 2 * R), np.float32)
    for t in range(R):
        for r in range(N):
            far = (r + 1 + t) % N
            q = mx_ref.quantize(now[r])
            s = mx_ref.matmul(qu[r], q) + np.float32(0.0)
            turn = np.where(parts(s[2::16] > 0), np.float32(1.0), np.float32(-1.0))
            fold = (decode(q) * turn).astype(BF)
            own = now[r].astype(np.float32) * turn
            back = []
            for k in range(2):
                b = 1 + np.argmax(s[k::16, 1:E], axis=1)
                od[r, :, 2 * t + k] = b
                low = np.stack([place[place < place ^ j] for j in b])
                i = np.take_along_axis(at[r][:, 2 * t + k], low, axis=1)
                m = np.take_along_axis(at[r][:, 2 * t + k], low ^ b[:, None], axis=1)
                z = mx_ref.quantize(((gcols(fold, i).astype(np.float32) + gcols(fold, m).astype(np.float32)) * np.float32(0.5)).astype(BF))
                h = mx_ref.quantize(tile([mx_ref.matmul(pick(lay[far][k], np.arange(128 * j, 128 * j + 128)), z) * np.float32(0.03125) for j in range(4)]))
                n = np.zeros((8, C), int)
                for e in (i, m): np.put_along_axis(n, e, np.broadcast_to(np.arange(C // 2), (8, C // 2)), axis=1)
                back.append(gcols(decode(h).astype(BF), n).astype(np.float32))
            middle = np.maximum(np.minimum(back[0], back[1]), np.minimum(np.maximum(back[0], back[1]), own))
            now[r] = ((own + middle) * np.float32(0.5)).astype(BF)
    y = np.zeros((N, 128, C), np.float32)
    oc, osc = np.zeros((N, 128, 4 * C), np.uint8), np.zeros((N, 16, C), np.uint8)
    for r in range(N):
        q = mx_ref.quantize(now[r])
        y[r] = mx_ref.matmul(mx_ref.quantize(v[r]), q)
        oc[r], osc[r] = emit(q)
    return {"y": y, "od": od, "oc": oc, "osc": osc}

@@ -1,0 +1,495 @@
+from concourse.mybir import dt, AluOpType, AxisListType, ActivationFunctionType
+
+C, P2, R = 192, 96, 3
+X4, U8, U16, BF, F32, I32 = "float8_e4m3fn_x4", "uint8", "uint16", "bfloat16", "float32", "int32"
+NSEG = 4 * R
+XP = 256
+OPT = {"early": True}
+
+SCRATCH = {
+    "ub": ("sbuf", [128, 512], BF), "vb": ("sbuf", [128, 512], BF), "pli": ("sbuf", [128, 72], I32),
+    "w0c": ("sbuf", [128, 512], X4), "w0s": ("sbuf", [128, 512], U8),
+    "w1c": ("sbuf", [128, 512], X4), "w1s": ("sbuf", [128, 512], U8),
+    "uc": ("sbuf", [128, 128], X4), "us": ("sbuf", [128, 128], U8),
+    "upc": ("sbuf", [128, 256], X4), "ups": ("sbuf", [128, 256], U8),
+    "vc": ("sbuf", [128, 128], X4), "vs": ("sbuf", [128, 128], U8),
+    "tl": ("sbuf", [128, 4 * C + 4 * P2 * NSEG], BF), "xs": ("sbuf", [128, XP + 4 * C * R], BF),
+    "lc": ("sbuf", [128, C + P2 * NSEG], X4), "ls": ("sbuf", [128, C + P2 * NSEG], U8),
+    "sc": ("sbuf", [128, 128 * NSEG], X4), "ss": ("sbuf", [128, 128 * NSEG], U8),
+    "qc": ("sbuf", [128, C * R], X4), "qs": ("sbuf", [128, C * R], U8),
+    "dc": ("sbuf", [128, 128 * R], X4), "ds": ("sbuf", [128, 128 * R], U8),
+    "jj": ("sbuf", [128, 128], BF), "ef": ("sbuf", [128, 520], BF), "hf": ("sbuf", [128, 520], BF),
+    "ec": ("sbuf", [128, 512], X4), "es": ("sbuf", [128, 512], U8),
+    "hc": ("sbuf", [128, 512], X4), "hs": ("sbuf", [128, 512], U8),
+    "pi": ("sbuf", [128, 8], I32), "ai": ("sbuf", [128, 16], I32), "af": ("sbuf", [128, 16], F32),
+    "tmp": ("sbuf", [128, 64], F32), "tmi": ("sbuf", [128, 8], I32), "ones": ("sbuf", [128, 64], F32),
+    "io1": ("sbuf", [128, 48], F32), "slot": ("sbuf", [128, C], BF), "cnt": ("sbuf", [128, C], BF),
+    "dlt": ("sbuf", [128, 64], F32), "tab": ("sbuf", [128, 512], F32),
+    "ul": ("sbuf", [128, 16], U16), "prl": ("sbuf", [128, 16], U16), "fnl": ("sbuf", [128, 2], U16),
+    "stl": ("sbuf", [128, 24], U16),
+    "plf": ("sbuf", [128, 72], F32), "pre": ("sbuf", [128, 256 * R], BF), "win": ("sbuf", [128, 256 * R], BF),
+    "mxv": ("sbuf", [128, 8], F32), "ltv": ("sbuf", [128, 64 * R], F32), "stv": ("sbuf", [128, 64 * R], F32),
+    "of0": ("sbuf", [128, 8], U16), "g0": ("sbuf", [128, 16 * R], U16),
+    "g1": ("sbuf", [128, 128 * R], F32), "g1t": ("sbuf", [128, 128 * R], F32), "fw": ("sbuf", [128, 32 * R], U16),
+    "inv0": ("sbuf", [128, 208], BF), "inv1": ("sbuf", [128, 208], BF), "fd": ("sbuf", [128, 24 * R], U16),
+    "nw": ("sbuf", [128, 768 * R], BF), "ntr": ("sbuf", [128, 768 * R], BF),
+    "n24": ("sbuf", [128, 32 * R], F32), "bl": ("sbuf", [128, 48 * R], U16),
+    "bt": ("sbuf", [128, 32], F32), "btt": ("sbuf", [128, 32], F32), "odt": ("sbuf", [128, 4], F32),
+    "sg": ("sbuf", [128, C * R], F32), "vv": ("sbuf", [128, 4 * C * R], BF), "lo": ("sbuf", [128, 4 * C * R], BF),
+    "yh": ("sbuf", [128, 4 * C * R], BF), "yp": ("sbuf", [128, 4 * C * R], BF), "dh": ("sbuf", [128, 4 * P2 * R], BF),
+    "pp": ("sbuf", [128, 4 * C * R], BF), "qq": ("sbuf", [128, 4 * C * R], BF),
+    "rr": ("sbuf", [128, 4 * C * R], BF), "mm": ("sbuf", [128, 4 * C * R], BF),
+    "yo": ("sbuf", [128, C], F32),
+}
+for _b in range(8):
+    SCRATCH["ps%d" % _b] = ("psum", [128, 512], F32)
+
+LOADS = ["pl", "u", "x", "wc", "ws", "mc", "ms", "v"]
+SEMAPHORES = (["eV", "eA", "eP", "eG", "sent", "st"] + ["ld_" + n for n in LOADS] + ["arr%d" % s for s in range(NSEG)])
+
+
+def emit(ops, queues, T, finals, landing):
+    writer, readers = {}, {}
+    clock = {q: {} for q in queues}
+    count = {q: 0 for q in queues}
+    done = {}
+    needed = set()
+    plan = []
+    for eng, fn, rd, wr, tok in ops:
+        deps = []
+        for k in rd:
+            if k in writer: deps.append(writer[k])
+            if k[0] == "arr": deps.append(("arr%d" % k[1], landing[k[1]]))
+            if k[0] == "ps": deps += [t for t in readers.get(k, []) if t[0] != eng]
+        for k in wr:
+            if k in writer: deps.append(writer[k])
+            deps += readers.get(k, [])
+        want = {}
+        for s, i in deps:
+            want[s] = max(want.get(s, 0), i)
+        waits = []
+        for s in sorted(want, key=lambda s: -len(done.get((s, want[s]), {}))):
+            if clock[eng].get(s, 0) >= want[s]: continue
+            waits.append((s, want[s]))
+            needed.add((s, want[s]))
+            clock[eng][s] = want[s]
+            for a, b in done.get((s, want[s]), {}).items():
+                clock[eng][a] = max(clock[eng].get(a, 0), b)
+        if tok is None:
+            count[eng] += 1
+            me = (eng, count[eng])
+        else:
+            me = tok
+        done[me] = dict(clock[eng])
+        for k in rd: readers.setdefault(k, []).append(me)
+        for k in wr:
+            writer[k] = me
+            readers[k] = []
+        plan.append((eng, fn, waits, me, tok))
+    value, total = {}, {q: 0 for q in queues}
+    for eng, fn, waits, me, tok in plan:
+        if tok is None and me in needed:
+            total[eng] += 1
+            value[me] = total[eng]
+    for eng, fn, waits, me, tok in plan:
+        for s, i in waits:
+            if s in queues: queues[eng].wait_ge(T.sem["e" + s], value[(s, i)])
+            else: queues[eng].wait_ge(T.sem[s], i)
+        ins = fn()
+        if tok is None:
+            if me in needed: ins.then_inc(T.sem["e" + eng], 1)
+        elif tok[0] != "remote":
+            ins.then_inc(T.sem[tok[0]], 16)
+    for s, v in finals:
+        queues["G"].wait_ge(T.sem[s], v)
+
+
+def rank_program(g, core, T, topo):
+    rank = T.rank_of(core)
+    if rank is None:
+        return
+    n_ranks = len(T.cores)
+    A = AluOpType
+    ID, CP = ActivationFunctionType.Identity, ActivationFunctionType.Copy
+    vec, act, pe, syn = g.vector, g.scalar, g.tensor, g.sync
+    queues = {"V": vec, "A": act, "P": pe, "G": g, "S": syn}
+    ops = []
+    stores, sent, landing = [0], [0], {}
+
+    def op(eng, fn, rd, wr, tok=None):
+        ops.append((eng, fn, [k if isinstance(k, tuple) else (k,) for k in rd], [k if isinstance(k, tuple) else (k,) for k in wr], tok))
+
+    def ts(out, in0, s1, s2, o0, o1, rd, wr):
+        if s2 is None: op("V", lambda: vec.tensor_scalar(out, in0, s1, None, o0), rd, wr)
+        else: op("V", lambda: vec.tensor_scalar(out, in0, s1, s2, o0, o1), rd, wr)
+
+    def tt(out, in0, in1, o, rd, wr): op("V", lambda: vec.tensor_tensor(out, in0, in1, o), rd, wr)
+    def cp(out, in_, rd, wr): op("V", lambda: vec.tensor_copy(out, in_), rd, wr)
+    def ms(out, c, wr): op("V", lambda: vec.memset(out, c), [], wr)
+    def tr(out, in_, rd, wr): op("V", lambda: vec.transpose(out, in_), rd, wr)
+    def qz(oc, os_, in_, rd, wr): op("V", lambda: vec.quantize_mx(oc, os_, in_), rd, wr)
+    def scan(out, d0, d1, init, o0, o1, rd, wr): op("V", lambda: vec.tensor_tensor_scan(out, d0, d1, init, o0, o1), rd, wr)
+    def acp(out, in_, rd, wr): op("A", lambda: act.activation(out, in_, CP), rd, wr)
+    def asc(out, in_, s, rd, wr): op("A", lambda: act.activation(out, in_, CP, scale=s), rd, wr)
+    def aff(out, in_, s, b, rd, wr): op("A", lambda: act.activation(out, in_, ID, bias=b, scale=s), rd, wr)
+    def mm(out, lc_, ls_, rc, rs, rd, wr): op("P", lambda: pe.matmul_mx(out, lc_, ls_, rc, rs, True, True), rd, wr)
+    def iota(out, pat, base, cm, wr, small=True):
+        if small: op("G", lambda: g.iota(out, pat, base, cm, allow_small_or_imprecise_dtypes=True), [], wr)
+        else: op("G", lambda: g.iota(out, pat, base, cm), [], wr)
+    def load(eng, out, name): op(eng, lambda: queues[eng].dma_start(out, T[name][:]), [], ["in_" + name], ("ld_" + name, 16))
+    def store(eng, out, in_, rd):
+        stores[0] += 16
+        op(eng, lambda: queues[eng].dma_start(out, in_), rd, [], ("st", stores[0]))
+    def ps(b): return T["ps%d" % b]
+
+    def send(seg, to, frm):
+        rid, pid, _ = topo.addr(to)
+        mask = topo.mask(core, to)
+        a, l = 128 * seg + 32, C + P2 * seg
+        sent[0] += 2 * len(topo.engines(core, to))
+        landing[seg] = 2 * len(topo.engines(frm, core))
+        op("G", lambda: g.remote_dma(T.lc[:, l:l + P2].bitcast(dt.uint8), T.sc[:, a:a + P2].bitcast(dt.uint8),
+                                     T.sem["arr%d" % seg], T.sem.sent, pid, rid, mask), [("sc", seg)], [], ("remote", 2 * seg + 1))
+        op("G", lambda: g.remote_dma(T.ls[:, l:l + P2], T.ss[:, a:a + P2],
+                                     T.sem["arr%d" % seg], T.sem.sent, pid, rid, mask), [("sc", seg)], [], ("remote", 2 * seg + 2))
+
+    def tile_keys(seg): return [("tl", seg, b) for b in range(4)] if seg >= 0 else ["in_x"]
+
+    def quant_piece(seg):
+        e = 4 * C + 4 * P2 * (seg + 1)
+        qz(T.sc[:, 128 * seg:128 * seg + 128], T.ss[:, 128 * seg:128 * seg + 128], T.tl[:, e - 512:e],
+           tile_keys(seg) + tile_keys(seg - 1), [("sc", seg)])
+
+    def landed(seg):
+        e = C + P2 * (seg + 1)
+        return T.lc[:, e - 128:e], T.ls[:, e - 128:e], [("arr", seg), ("arr", seg - 1) if seg > 0 else ("qx", 0)]
+
+    def qx(t, n=C):
+        return (T.lc[:, 0:n], T.ls[:, 0:n]) if t == 0 else (T.qc[:, C * (t - 1):C * (t - 1) + n], T.qs[:, C * (t - 1):C * (t - 1) + n])
+
+    def xcol(t, b, c0=0, c1=C):
+        o = XP + 4 * C * (t - 1)
+        return T.tl[:, b:4 * C:4] if t == 0 else T.xs[:, o + 4 * c0 + b:o + 4 * c1:4]
+
+    def xkeys(t, parts=(0, 1)): return ["in_x"] if t == 0 else [("xs", t, b, c) for b in range(4) for c in parts]
+
+    load("S", T.pli[:], "pl")
+    load("A", T.ub[:], "u")
+    load("S", T.tl[:, 0:4 * C], "x")
+    load("S", T.w0c[:].bitcast(dt.uint8), "wc")
+    load("S", T.w0s[:], "ws")
+    load("S", T.w1c[:].bitcast(dt.uint8), "mc")
+    load("S", T.w1s[:], "ms")
+    load("S", T.vb[:], "v")
+
+    iota(T.pi[:, 0:1], [[0, 1]], 0, 1, ["pi0"], small=False)
+    iota(T.pi[:, 1:2], [[0, 1]], 0, 2, ["pi1"], small=False)
+    iota(T.jj[:], [[1, 128]], 0, -1, ["jj"])
+    iota(T.io1[:, 0:8], [[32, 4], [0, 2]], 0, 0, ["io_u"])
+    iota(T.io1[:, 8:16], [[16, 8]], 2, 0, ["io_u2"])
+    iota(T.io1[:, 16:32], [[12, 2], [1, 4], [0, 2]], 0, 0, ["io_p"])
+    iota(T.io1[:, 32:44], [[16, 12]], 0, 0, ["io_n"])
+    iota(T.slot[:], [[0, 2], [1, P2]], 0, 0, ["slot"])
+    iota(T.cnt[:], [[1, C]], 0, 0, ["cnt"])
+
+    ms(T.ef[:], 0.0, ["ef"])
+    ms(T.ones[:], 1.0, ["ones"])
+    ms(T.dlt[:, 0:1], 0.0, [("dlt", 0)])
+    WT = [1, 2, 4, 8, 32, 64]
+    for col, src, m in ((0, 0, 1), (1, 0, 2), (2, 0, 4), (3, 0, 8), (8, 0, 15), (9, 0, 16), (4, 1, 32), (6, 1, 63), (7, 1, 48)):
+        ts(T.ai[:, col:col + 1], T.pi[:, src:src + 1], m, None, A.bitwise_and, None, ["pi%d" % src], [("ai", col)])
+    cp(T.af[:, 0:5], T.ai[:, 0:5], [("ai", c) for c in range(5)], ["af"])
+    cp(T.af[:, 6:10], T.ai[:, 6:10], [("ai", c) for c in range(6, 10)], ["af2"])
+    af = lambda c: T.af[:, c:c + 1]
+    tm = lambda c: T.tmp[:, c:c + 1]
+
+    def double(s):
+        w = 1 << s
+        rd = [("dlt", i) for i in range(s + 1)]
+        if s < 5: ts(T.dlt[:, w:2 * w], T.dlt[:, 0:w], float(WT[s]), tm(40 + s), A.add, A.subtract, rd + ["a2"], [("dlt", s + 1)])
+        else: ts(T.dlt[:, w:2 * w], T.dlt[:, 0:w], float(WT[s]), None, A.add, None, rd, [("dlt", s + 1)])
+
+    def qe(b): qz(T.ec[:, 128 * b:128 * b + 128], T.es[:, 128 * b:128 * b + 128], T.ef[:, 3 - b:515 - b], ["ef"], [("e", b)])
+
+    ts(T.tmp[:, 40:45], T.af[:, 0:5], 2.0, None, A.mult, None, ["af"], ["a2"])
+    cp(T.tmp[:, 8:13], T.af[:, 0:5], ["af"], ["dd"])
+    tt(tm(0), af(6), af(7), A.add, ["af2"], ["lo0"])
+    double(0)
+    ts(tm(11), af(3), 3.0, None, A.mult, None, ["af", "dd"], ["dd"])
+    double(1)
+    ts(T.ef[:, 3:515:4], T.jj[:], 0.0, None, A.is_equal, None, ["jj", "ef"], ["ef"])
+    scan(T.tmp[:, 1:6], T.ones[:, 0:5], T.tmp[:, 8:13], tm(0), A.mult, A.subtract, ["ones", "dd", "lo0"], ["lo1"])
+    double(2)
+    ts(tm(34), af(8), 2.0, 4.0, A.min, A.mult, ["af2"], ["t34"])
+    tt(T.tmp[:, 16:21], T.tmp[:, 40:45], T.tmp[:, 0:5], A.add, ["a2", "lo0", "lo1"], ["cc"])
+    double(3)
+    qe(0)
+    double(4)
+    qe(1)
+    double(5)
+    ts(T.prl[:], T.io1[:, 16:32], tm(34), None, A.add, None, ["io_p", "t34"], ["prl"])
+    aff(tm(32), af(2), 0.25, 0.0, ["af"], ["t32"])
+    aff(tm(35), af(0), 128.0, 63.0, ["af"], ["t35"])
+    aff(tm(33), af(0), 16.0, tm(32), ["af", "t32"], ["t33"])
+    aff(tm(36), af(1), 32.0, tm(35), ["af", "t35"], ["t36"])
+    cp(T.ul[:, 8:16], T.io1[:, 8:16], ["io_u2"], ["ul2"])
+    ts(T.ul[:, 0:8], T.io1[:, 0:8], tm(33), None, A.add, None, ["io_u", "t33"], ["ul"])
+    for h in range(6):
+        a, w = (0, 2) if h == 0 else (1 << h, 2 << h)
+        aff(T.tab[:, a:w], T.ones[:, a:w], 0.0, tm(h), ["ones", "lo0", "lo1"], [("tab", 0, h)])
+    aff(tm(37), af(2), 64.0, tm(36), ["af", "t36"], ["cp"])
+    for h in range(6):
+        a, w = (0, 2) if h == 0 else (1 << h, 2 << h)
+        rd = [("dlt", i) for i in range(h + 2)] + ["cc", "lo1"]
+        if h < 3: aff(T.tab[:, 64 + a:64 + w], T.dlt[:, a:w], 1.0, tm(16 + h), rd, [("tab", 1, h)])
+        else: ts(T.tab[:, 64 + a:64 + w], T.dlt[:, a:w], tm(16 + h) if h < 5 else tm(5), None, A.add, None, rd, [("tab", 1, h)])
+    cp(T.plf[:], T.pli[:], ["in_pl"], ["plf"])
+
+    def windows(t):
+        acp(T.pre[:, 256 * t:256 * t + 256], T.plf[:, 24 * t:24 * t + 24].indirect(T.prl[:]), ["plf", "prl"], [("pre", t)])
+
+    def windows2(t):
+        tr(T.win[:, 256 * t:256 * t + 256], T.pre[:, 256 * t:256 * t + 256], [("pre", t)], [("win", t)])
+
+    tabs = [("tab", i, h) for i in range(2) for h in range(6)]
+    qe(2)
+    qe(3)
+    qz(T.uc[:], T.us[:], T.ub[:], ["in_u"], ["uq"])
+    aff(T.tab[:, 128:256], T.tab[:, 0:128], 1.0, 16.0, tabs, ["tab1"])
+    acp(T.ups[:, 0:128], T.us[:].indirect(T.ul[:, 0:8]), ["uq", "ul"], ["ups0"])
+    qz(T.lc[:, 0:C], T.ls[:, 0:C], T.tl[:, 0:4 * C], ["in_x"], [("qx", 0)])
+    cp(T.upc[:, 0:128].bitcast(dt.uint32), T.uc[:].bitcast(dt.uint32).indirect(T.ul[:, 0:8]), ["uq", "ul"], ["upc0"])
+    cp(T.upc[:, 128:256].bitcast(dt.uint32), T.uc[:].bitcast(dt.uint32).indirect(T.ul[:, 8:16]), ["uq", "ul2"], ["upc1"])
+    acp(T.ups[:, 128:256], T.us[:].indirect(T.ul[:, 8:16]), ["uq", "ul2"], ["ups1"])
+    windows(0)
+    aff(T.tab[:, 256:512], T.tab[:, 0:256], 1.0, 128.0, tabs + ["tab1"], ["tab2"])
+    ts(T.tmp[:, 48:50], T.io1[:, 32:34], af(8), 23.0, A.add, A.min, ["io_n", "af2"], ["nn"])
+
+    def direction(t, bank, c0):
+        mx, lt, st = T.mxv[:, t:t + 1], T.ltv[:, 64 * t:64 * t + 63], T.stv[:, 64 * t:64 * t + 63]
+        last = T.stv[:, 64 * t + 62:64 * t + 63]
+        s = ps(bank)[:, c0 + 1:c0 + 64]
+        return [
+            lambda: op("V", lambda: vec.tensor_reduce(mx, s, AxisListType.X, A.max), [("ps", bank)], [("mx", t)]),
+            lambda: ts(lt, s, mx, -1000.0, A.is_lt, A.mult, [("ps", bank), ("mx", t)], [("lt", t)]),
+            lambda: scan(st, T.ones[:, 0:63], lt, -1000.0, A.add, A.max, ["ones", ("lt", t)], [("st", t)]),
+            lambda: ts(T.of0[:, 2 * t:2 * t + 1], last, -1.0, tm(37), A.mult, A.add, [("st", t), "cp"], [("of0", t)]),
+            lambda: (cp(T.g0[:, 16 * t:16 * t + 16], T.tab[:].indirect(T.of0[:, 2 * t:2 * t + 1]), tabs + ["tab1", "tab2", ("of0", t)], [("g0", t)]),
+                     acp(T.g1[:, 128 * t:128 * t + 128], T.win[:, 256 * t:256 * t + 256].indirect(T.g0[:, 16 * t:16 * t + 8]),
+                         [("win", t), ("g0", t)], [("g1", t)])),
+            lambda: tr(T.g1t[:, 128 * t:128 * t + 128], T.g1[:, 128 * t:128 * t + 128], [("g1", t)], [("g1t", t)]),
+            lambda: cp(T.fw[:, 32 * t:32 * t + 32], T.g1t[:, 128 * t:128 * t + 128].indirect(T.fnl[:, 0:2]),
+                       [("g1t", t), ("fnl", 0), ("fnl", 1)], [("fw", t)]),
+        ]
+
+    rest = []
+    for t in range(R):
+        lender = T.cores[(rank + 1 + t) % n_ranks]
+        borrower = T.cores[(rank - 1 - t) % n_ranks]
+        xc, xsc = qx(t)
+        o4, s0 = 4 * C * t, 4 * t
+        kq = [("qx", t)]
+        late = t == 0 or not OPT["early"]
+        if late:
+            xa = qx(t, 128)
+            mm(ps(0)[:, 0:128], T.upc[:, 0:128], T.ups[:, 0:128], xa[0], xa[1], kq + ["upc0", "ups0"], [("ps", 0)])
+            d = direction(t, 0, 0)
+        mm(ps(1)[:, 0:C], T.upc[:, 128:256], T.ups[:, 128:256], xc, xsc, kq + ["upc1", "ups1"], [("ps", 1)])
+        for b in range(4):
+            mm(ps(2 + b)[:, 0:C], T.ec[:, 128 * b:128 * b + 128], T.es[:, 128 * b:128 * b + 128], xc, xsc, kq + [("e", b)], [("ps", 2 + b)])
+        sgn = T.sg[:, C * t:C * t + C]
+
+        def sign(): ts(sgn, ps(1)[:, 0:C], 0.0, 0.5, A.is_gt, A.subtract, [("ps", 1)], [("sg", t)])
+
+        def vmul(b):
+            tt(T.vv[:, o4 + C * b:o4 + C * b + C], ps(2 + b)[:, 0:C], sgn, A.mult, [("ps", 2 + b), ("sg", t)], [("vv", t, b)])
+
+        def pair(k, b):
+            z0 = 4 * C + 4 * P2 * (s0 + k)
+            w = T.vv[:, o4 + C * b:o4 + C * b + C]
+            l = T.lo[:, o4 + 4 * P2 * k + P2 * b:o4 + 4 * P2 * k + P2 * b + P2]
+            f = 32 * t + 12 * k
+            return (lambda: acp(l, w.indirect(T.fw[:, f:f + 6]), [("vv", t, b), ("fw", t)], [("lo", t, k, b)]),
+                    lambda: tt(T.tl[:, z0 + b:z0 + 4 * P2:4], w.indirect(T.fw[:, f + 6:f + 12]), l, A.add,
+                               [("vv", t, b), ("fw", t), ("lo", t, k, b)], [("tl", s0 + k, b)]))
+
+        if late:
+            if t == 0: ts(T.tmp[:, 50:52], T.tmp[:, 48:50], 1.0 / 3.0, 1.0 / 3.0, A.mult, A.subtract, ["nn"], ["n3"])
+            d[0]()
+            if t == 0: cp(T.tmi[:, 0:2], T.tmp[:, 50:52], ["n3"], ["n3i"])
+            d[1]()
+            sign()
+            d[2]()
+            vmul(0)
+            d[3]()
+            vmul(1)
+            if t == 0: windows2(0)
+            d[4]()
+            vmul(2)
+            if t == 0:
+                for c in range(2):
+                    ts(T.fnl[:, c:c + 1], T.tmi[:, c:c + 1], 13.0, tm(48 + c), A.mult, A.add, ["n3i", "nn"], [("fnl", c)])
+            d[5]()
+            vmul(3)
+            d[6]()
+            for b in range(4):
+                for f in pair(0, b): f()
+        else:
+            rest[0]()
+            sign()
+            vmul(0)
+            rest[1]()
+            vmul(1)
+            rest[2]()
+            pr = [pair(0, b) for b in range(4)]
+            pr[0][0]()
+            pr[1][0]()
+            vmul(2)
+            vmul(3)
+            pr[2][0]()
+            pr[3][0]()
+            for b in range(4): pr[b][1]()
+        quant_piece(s0)
+        send(s0, lender, borrower)
+        for b in range(4):
+            for f in pair(1, b): f()
+        quant_piece(s0 + 1)
+        send(s0 + 1, lender, borrower)
+
+        def ymul(b):
+            tt(T.yh[:, o4 + C * b:o4 + C * b + C], xcol(t, b), sgn, A.mult, xkeys(t) + [("sg", t)], [("yh", t, b)])
+
+        def yperm(b):
+            a = o4 + C * b
+            acp(T.yp[:, a:a + C], T.yh[:, a:a + C].indirect(T.fw[:, 32 * t:32 * t + 12]), [("yh", t, b), ("fw", t)], [("yp", t, b)])
+
+        def lend(k):
+            rc, rs, keys = landed(s0 + k)
+            wc_, ws_, wk = (T.w0c, T.w0s, ["in_wc", "in_ws"]) if k == 0 else (T.w1c, T.w1s, ["in_mc", "in_ms"])
+            h0 = 4 * C + 4 * P2 * (s0 + 2 + k)
+            for b in range(4):
+                mm(ps(4 * k + b)[:, 0:128], wc_[:, 128 * b:128 * b + 128], ws_[:, 128 * b:128 * b + 128], rc, rs, keys + wk, [("ps", 4 * k + b)])
+            for b in range(4):
+                o, i = T.tl[:, h0 + b:h0 + 4 * P2:4], ps(4 * k + b)[:, 32:128]
+                if b % 2 == 0: asc(o, i, 0.03125, [("ps", 4 * k + b)], [("tl", s0 + 2 + k, b)])
+                else: ts(o, i, 0.03125, None, A.mult, None, [("ps", 4 * k + b)], [("tl", s0 + 2 + k, b)])
+            quant_piece(s0 + 2 + k)
+            send(s0 + 2 + k, borrower, lender)
+
+        n0 = 768 * t
+        if t == 0:
+            aff(tm(52), af(9), 1.0 / 16.0, 0.0, ["af2"], ["m1"])
+            aff(tm(53), af(9), -1.0 / 16.0, 1.0, ["af2"], ["m0"])
+            aff(tm(54), af(9), C / 16.0, 0.0, ["af2"], ["c0"])
+            aff(tm(55), af(9), -C / 16.0, float(C), ["af2"], ["c1"])
+        if t + 1 < R: windows(t + 1)
+        for b in range(4): ymul(b)
+        yperm(0)
+        yperm(1)
+        if t == 0:
+            ms(T.inv0[:], 0.0, ["z0", "inv0"])
+            ms(T.inv1[:], 0.0, ["z1", "inv1"])
+            ms(T.bt[:], 0.0, ["bt"])
+            ts(T.tmp[:, 20:32], T.io1[:, 32:44], af(8), None, A.add, None, ["io_n", "af2"], ["cc"])
+            ts(T.hf[:], T.ef[:], 0.5, None, A.mult, None, ["ef"], ["hf"])
+            for e in range(2):
+                ts(T.stl[:, e:24:2], T.tmp[:, 20:32], tm(53 - e), tm(54 + e), A.mult, A.add, ["cc", "m0", "m1", "c0", "c1"], [("stl", e)])
+            for b in range(4):
+                qz(T.hc[:, 128 * b:128 * b + 128], T.hs[:, 128 * b:128 * b + 128], T.hf[:, 3 - b:515 - b], ["hf"], [("h", b)])
+        for e in range(2):
+            ts(T.fd[:, 24 * t + e:24 * t + 24:2], T.fw[:, 32 * t:32 * t + 12], tm(53 - e), tm(54 + e), A.mult, A.add,
+               [("fw", t), "m0", "m1", "c0", "c1"], [("fd", t, e)])
+        ts(T.bt[:, t:t + 1], T.stv[:, 64 * t + 62:64 * t + 63], -1.0, 63.0, A.mult, A.add, [("st", t), "bt"], [("btc", t)])
+        if t + 1 < R: windows2(t + 1)
+        lend(0)
+        yperm(2)
+        cp(T.inv1[:, 0:C].indirect(T.fw[:, 32 * t + 12:32 * t + 24]), T.slot[:], ["slot", ("fw", t)], ["inv1"])
+        lend(1)
+        yperm(3)
+        acp(T.nw[:, n0 + 384:n0 + 768], T.inv1[:].indirect(T.fd[:, 24 * t:24 * t + 24]), ["inv1", "z1", ("fd", t, 0), ("fd", t, 1)], [("nw", t, 1)])
+        cp(T.inv0[:, 0:C].indirect(T.fw[:, 32 * t:32 * t + 12]), T.cnt[:], ["cnt", ("fw", t)], ["inv0"])
+        acp(T.nw[:, n0:n0 + 384], T.inv0[:].indirect(T.stl[:]), ["inv0", "z0", ("stl", 0), ("stl", 1)], [("nw", t, 0)])
+
+        def lists(k):
+            a = n0 + 384 * k
+            return [lambda: tr(T.ntr[:, a:a + 384], T.nw[:, a:a + 384], [("nw", t, k)], [("ntr", t, k)]),
+                    lambda: tt(T.n24[:, 32 * t + 12 * k:32 * t + 12 * k + 12], T.ntr[:, a:a + 384:32], T.ntr[:, a + 16:a + 384:32], A.add,
+                               [("ntr", t, k)], [("n24", t, k)])]
+
+        l0, l1 = lists(0), lists(1)
+        l1[0]()
+        if t == 0:
+            ms(T.xs[:, 0:XP], 0.0, [("xs", 0, b, 1) for b in range(4)])
+            qz(T.vc[:], T.vs[:], T.vb[:], ["in_v"], ["vq"])
+        l1[1]()
+        for e in range(2):
+            a = 48 * t + 12 * e
+            ts(T.bl[:, a:a + 12], T.n24[:, 32 * t + 12:32 * t + 24], float(P2 * e), None, A.add, None, [("n24", t, 1)], [("bl", t, e)])
+        l0[0]()
+        if t == R - 1:
+            tr(T.btt[:], T.bt[:], ["bt"] + [("btc", i) for i in range(R)], ["btt"])
+        l0[1]()
+        if t == R - 1:
+            for k in range(2):
+                cp(T.odt[:, k:4:2], T.btt[:, 4 * k:4 * k + 2], ["btt"], [("odt", k)])
+            for gr in range(8):
+                store("S", T.od[gr:gr + 1, :], T.odt[32 * (gr // 2):32 * (gr // 2) + R, 2 * (gr % 2):2 * (gr % 2) + 2], [("odt", 0), ("odt", 1)])
+        cp(T.bl[:, 48 * t + 24:48 * t + 36], T.n24[:, 32 * t:32 * t + 12], [("n24", t, 0)], [("bl", t, 2)])
+        for k in range(2):
+            rc, rs, keys = landed(s0 + 2 + k)
+            for b in range(4):
+                mm(ps(4 * k + b)[:, 0:128], T.hc[:, 128 * b:128 * b + 128], T.hs[:, 128 * b:128 * b + 128], rc, rs, keys + [("h", b)], [("ps", 4 * k + b)])
+        for b in range(4):
+            a = 4 * P2 * t + P2 * b
+            acp(T.dh[:, a:a + P2], ps(4 + b)[:, 32:128], [("ps", 4 + b)], [("dh", t, b)])
+        for b in range(4):
+            for e in range(2):
+                a = o4 + C * b + P2 * e
+                tt(T.qq[:, a:a + P2], ps(b)[:, 32:128], T.yp[:, a:a + P2], A.max, [("ps", b), ("yp", t, b)], [("qq", t, b, e)])
+                tt(T.pp[:, a:a + P2], ps(b)[:, 32:128], T.yp[:, a:a + P2], A.min, [("ps", b), ("yp", t, b)], [("pp", t, b, e)])
+        half = lambda buf, c: buf[:, o4 + 2 * C * c:o4 + 2 * C * (c + 1)]
+        both = lambda n, c: [(n, t, 2 * c + i, e) for i in range(2) for e in range(2)]
+        for c in range(2):
+            a = 4 * P2 * t + 2 * P2 * c
+            tt(half(T.rr, c), T.dh[:, a:a + 2 * P2].indirect(T.bl[:, 48 * t:48 * t + 24]), half(T.qq, c), A.min,
+               [("dh", t, 2 * c), ("dh", t, 2 * c + 1), ("bl", t, 0), ("bl", t, 1)] + both("qq", c), [("rr", t, c)])
+        for c in range(2):
+            tt(half(T.mm, c), half(T.pp, c), half(T.rr, c), A.max, both("pp", c) + [("rr", t, c)], [("mm", t, c)])
+
+        def add(b, c0, c1, parts):
+            a, l = o4 + C * b, 48 * t + 24
+            tt(xcol(t + 1, b, c0, c1), T.mm[:, a:a + C].indirect(T.bl[:, l + c0 // 16:l + c1 // 16]), T.yh[:, a + c0:a + c1], A.add,
+               [("mm", t, b // 2), ("yh", t, b), ("bl", t, 2)], [("xs", t + 1, b, c) for c in parts])
+
+        if OPT["early"] and t + 1 < R:
+            for b in range(4): add(b, 0, 64, (0,))
+            e = XP + o4 + 256
+            qz(T.dc[:, 128 * t:128 * t + 128], T.ds[:, 128 * t:128 * t + 128], T.xs[:, e - 512:e],
+               xkeys(t + 1, (0,)) + [("xs", t, b, 1) for b in range(4)], [("dq", t)])
+            mm(ps(0)[:, 0:128], T.upc[:, 0:128], T.ups[:, 0:128], T.dc[:, 128 * t:128 * t + 128], T.ds[:, 128 * t:128 * t + 128],
+               [("dq", t), "upc0", "ups0"], [("ps", 0)])
+            d = direction(t + 1, 0, 64)
+            add(0, 64, C, (1,))
+            d[0]()
+            add(1, 64, C, (1,))
+            d[1]()
+            add(2, 64, C, (1,))
+            d[2]()
+            add(3, 64, C, (1,))
+            d[3]()
+            rest = d[4:]
+        else:
+            for b in range(4): add(b, 0, C, (0, 1))
+        nc, ns = qx(t + 1)
+        qz(nc, ns, T.xs[:, XP + o4:XP + o4 + 4 * C], xkeys(t + 1), [("qx", t + 1)])
+
+    xc, xsc = qx(R)
+    kq = [("qx", R)]
+    mm(ps(0)[:, 0:C], T.vc[:], T.vs[:], xc, xsc, kq + ["vq"], [("ps", 0)])
+    store("S", T.oc[:, :], xc.bitcast(dt.uint8), kq)
+    c0 = C * (R - 1)
+    for i in range(4):
+        store("A" if i == 3 else "S", T.osc[4 * i:4 * i + 4, :], T.qs[32 * i:32 * i + 4, c0:c0 + C], kq)
+    cp(T.yo[:], ps(0)[:, 0:C], [("ps", 0)], ["yo"])
+    store("A", T.y[:, :], T.yo[:], ["yo"])
+    emit(ops, queues, T, [("sent", sent[0]), ("st", stores[0])], landing)

@@ -3,43 +3,52 @@ from concourse.mybir import dt, AluOpType, AxisListType, ActivationFunctionType
 C, P2, R = 192, 96, 3
 X4, U8, U16, BF, F32, I32 = "float8_e4m3fn_x4", "uint8", "uint16", "bfloat16", "float32", "int32"
 NSEG = 4 * R
+W2 = 2 * C
 XP = 256
-OPT = {"early": True}
+BIG, HALF = 16 * (64 + 6), 576
+LOW = -1.0e29
+TINY = 2.0 ** -120
+OPT = {"aev": (), "adh": 1, "vlo": False, "pre": 3, "sfirst": False, "ash": False, "plq": "S", "ca": 64, "ball": False, "afill": True,
+       "start": "c0 c1 e0 c2 x0 p0 x1 u0 x2 e1 x3 u1 x4 p1 e2 p2 e3 p3 l0 l1 l2 l3 l4 l5 u2 h0 h1 u3 u4 p4 u5 h2 h3 u7 u6 p5 m0 s0 "
+                "h4 d0 h5 d1 c3 d2 c4 d3 p6 d4 v0 d5 v1 d6 d7 v2 v3",
+       "back": "o0 o1 o2 f0 b0 f1 f2 b1 f3 b2 b3 o3 m0 m1 m2 h1 m3 G0 g1 g2 g3 h2 h0 h3",
+       "wait": ["w1 k0 c1 c0 s0 W1 k1 i1 k2 k3 k4 n0 y0 p0 a0 y1 p1 a1 y2 p2 a2 t0 k8 k5 L0 L1 y3 p3 t1 i0 T0 k6 k9 r0 k7 r1 b0 T1 l1 l0",
+                "w2 c1 c0 s0 W2 i1 n0 y0 p0 y1 p1 y2 p2 t0 L0 L1 y3 p3 t1 i0 T0 r0 r1 b0 T1 l1 l0",
+                "c1 c0 s0 i1 n0 y0 p0 y1 p1 y2 p2 L0 L1 y3 p3 i0 r0 r1 b0 v0 l1 l0 d0 d1"],
+       "seq": "s0 a1 a2 d0 a3 d1 q0 d2 d3 v0 d4 d5 v1 v2 d6 v3 w0 w1 w2 w3"}
 
 SCRATCH = {
     "ub": ("sbuf", [128, 512], BF), "vb": ("sbuf", [128, 512], BF), "pli": ("sbuf", [128, 72], I32),
     "w0c": ("sbuf", [128, 512], X4), "w0s": ("sbuf", [128, 512], U8),
     "w1c": ("sbuf", [128, 512], X4), "w1s": ("sbuf", [128, 512], U8),
     "uc": ("sbuf", [128, 128], X4), "us": ("sbuf", [128, 128], U8),
-    "upc": ("sbuf", [128, 256], X4), "ups": ("sbuf", [128, 256], U8),
+    "upc": ("sbuf", [128, 384], X4), "ups": ("sbuf", [128, 384], U8),
     "vc": ("sbuf", [128, 128], X4), "vs": ("sbuf", [128, 128], U8),
     "tl": ("sbuf", [128, 4 * C + 4 * P2 * NSEG], BF), "xs": ("sbuf", [128, XP + 4 * C * R], BF),
     "lc": ("sbuf", [128, C + P2 * NSEG], X4), "ls": ("sbuf", [128, C + P2 * NSEG], U8),
     "sc": ("sbuf", [128, 128 * NSEG], X4), "ss": ("sbuf", [128, 128 * NSEG], U8),
     "qc": ("sbuf", [128, C * R], X4), "qs": ("sbuf", [128, C * R], U8),
-    "dc": ("sbuf", [128, 128 * R], X4), "ds": ("sbuf", [128, 128 * R], U8),
-    "jj": ("sbuf", [128, 128], BF), "ef": ("sbuf", [128, 520], BF), "hf": ("sbuf", [128, 520], BF),
+    "dc": ("sbuf", [128, C * R], X4), "ds": ("sbuf", [128, C * R], U8),
+    "jj": ("sbuf", [128, 128], BF), "ef": ("sbuf", [128, 520], BF),
     "ec": ("sbuf", [128, 512], X4), "es": ("sbuf", [128, 512], U8),
-    "hc": ("sbuf", [128, 512], X4), "hs": ("sbuf", [128, 512], U8),
     "pi": ("sbuf", [128, 8], I32), "ai": ("sbuf", [128, 16], I32), "af": ("sbuf", [128, 16], F32),
-    "tmp": ("sbuf", [128, 64], F32), "tmi": ("sbuf", [128, 8], I32), "ones": ("sbuf", [128, 64], F32),
-    "io1": ("sbuf", [128, 48], F32), "slot": ("sbuf", [128, C], BF), "cnt": ("sbuf", [128, C], BF),
-    "dlt": ("sbuf", [128, 64], F32), "tab": ("sbuf", [128, 512], F32),
-    "ul": ("sbuf", [128, 16], U16), "prl": ("sbuf", [128, 16], U16), "fnl": ("sbuf", [128, 2], U16),
-    "stl": ("sbuf", [128, 24], U16),
+    "tmp": ("sbuf", [128, 96], F32), "ones": ("sbuf", [128, 64], F32),
+    "sl": ("sbuf", [128, 8], U16), "bgl": ("sbuf", [128, 80], U16), "pw2": ("sbuf", [128, 64], F32), "stw": ("sbuf", [128, 64 * R + 64], F32), "big": ("sbuf", [128, BIG], BF), "bigt": ("sbuf", [128, BIG], BF),
+    "io1": ("sbuf", [128, 56], F32), "cnt": ("sbuf", [128, C], BF),
+    "dlt": ("sbuf", [128, 40], F32), "tab": ("sbuf", [128, 384], F32),
+    "ul": ("sbuf", [128, 24], U16), "prl": ("sbuf", [128, 16], U16), "gl": ("sbuf", [128, 2], U16),
     "plf": ("sbuf", [128, 72], F32), "pre": ("sbuf", [128, 256 * R], BF), "win": ("sbuf", [128, 256 * R], BF),
-    "mxv": ("sbuf", [128, 8], F32), "ltv": ("sbuf", [128, 64 * R], F32), "stv": ("sbuf", [128, 64 * R], F32),
+    "mxv": ("sbuf", [128, 8], F32), "ltv": ("sbuf", [128, 64 * R + 64], F32), "stv": ("sbuf", [128, 64 * R + 64], F32),
     "of0": ("sbuf", [128, 8], U16), "g0": ("sbuf", [128, 16 * R], U16),
-    "g1": ("sbuf", [128, 128 * R], F32), "g1t": ("sbuf", [128, 128 * R], F32), "fw": ("sbuf", [128, 32 * R], U16),
-    "inv0": ("sbuf", [128, 208], BF), "inv1": ("sbuf", [128, 208], BF), "fd": ("sbuf", [128, 24 * R], U16),
-    "nw": ("sbuf", [128, 768 * R], BF), "ntr": ("sbuf", [128, 768 * R], BF),
-    "n24": ("sbuf", [128, 32 * R], F32), "bl": ("sbuf", [128, 48 * R], U16),
+    "g1": ("sbuf", [128, 64 * R], BF), "g1t": ("sbuf", [128, 64 * R], BF), "fw": ("sbuf", [128, 64 * R], U16),
+    "fy": ("sbuf", [128, 24 * R], U16), "iv": ("sbuf", [128, 416], BF), "inv1": ("sbuf", [128, C], BF),
+    "cn2": ("sbuf", [128, C], BF), "ivt": ("sbuf", [128, 800], BF), "bl": ("sbuf", [128, 32 * R], U16),
     "bt": ("sbuf", [128, 32], F32), "btt": ("sbuf", [128, 32], F32), "odt": ("sbuf", [128, 4], F32),
-    "sg": ("sbuf", [128, C * R], F32), "vv": ("sbuf", [128, 4 * C * R], BF), "lo": ("sbuf", [128, 4 * C * R], BF),
+    "sg": ("sbuf", [128, C * R], BF), "sh": ("sbuf", [128, C * R], BF),
+    "vv": ("sbuf", [128, 4 * C * R], BF), "lo": ("sbuf", [128, 4 * C * R], BF),
     "yh": ("sbuf", [128, 4 * C * R], BF), "yp": ("sbuf", [128, 4 * C * R], BF), "dh": ("sbuf", [128, 4 * P2 * R], BF),
-    "pp": ("sbuf", [128, 4 * C * R], BF), "qq": ("sbuf", [128, 4 * C * R], BF),
-    "rr": ("sbuf", [128, 4 * C * R], BF), "mm": ("sbuf", [128, 4 * C * R], BF),
-    "yo": ("sbuf", [128, C], F32),
+    "pq": ("sbuf", [128, 4 * W2 * R], BF), "ad": ("sbuf", [128, 4 * W2], BF), "mo": ("sbuf", [128, 4 * W2 * R], BF),
+    "mc2": ("sbuf", [128, 4 * C], BF), "yo": ("sbuf", [128, C], F32),
 }
 for _b in range(8):
     SCRATCH["ps%d" % _b] = ("psum", [128, 512], F32)
@@ -110,7 +119,7 @@ def rank_program(g, core, T, topo):
         return
     n_ranks = len(T.cores)
     A = AluOpType
-    ID, CP = ActivationFunctionType.Identity, ActivationFunctionType.Copy
+    ID, CP, SG = ActivationFunctionType.Identity, ActivationFunctionType.Copy, ActivationFunctionType.Sign
     vec, act, pe, syn = g.vector, g.scalar, g.tensor, g.sync
     queues = {"V": vec, "A": act, "P": pe, "G": g, "S": syn}
     ops = []
@@ -136,7 +145,7 @@ def rank_program(g, core, T, topo):
     def iota(out, pat, base, cm, wr, small=True):
         if small: op("G", lambda: g.iota(out, pat, base, cm, allow_small_or_imprecise_dtypes=True), [], wr)
         else: op("G", lambda: g.iota(out, pat, base, cm), [], wr)
-    def load(eng, out, name): op(eng, lambda: queues[eng].dma_start(out, T[name][:]), [], ["in_" + name], ("ld_" + name, 16))
+    def load(eng, out, name, rd=()): op(eng, lambda: queues[eng].dma_start(out, T[name][:]), list(rd), ["in_" + name], ("ld_" + name, 16))
     def store(eng, out, in_, rd):
         stores[0] += 16
         op(eng, lambda: queues[eng].dma_start(out, in_), rd, [], ("st", stores[0]))
@@ -148,21 +157,25 @@ def rank_program(g, core, T, topo):
         a, l = 128 * seg + 32, C + P2 * seg
         sent[0] += 2 * len(topo.engines(core, to))
         landing[seg] = 2 * len(topo.engines(frm, core))
-        op("G", lambda: g.remote_dma(T.lc[:, l:l + P2].bitcast(dt.uint8), T.sc[:, a:a + P2].bitcast(dt.uint8),
-                                     T.sem["arr%d" % seg], T.sem.sent, pid, rid, mask), [("sc", seg)], [], ("remote", 2 * seg + 1))
-        op("G", lambda: g.remote_dma(T.ls[:, l:l + P2], T.ss[:, a:a + P2],
-                                     T.sem["arr%d" % seg], T.sem.sent, pid, rid, mask), [("sc", seg)], [], ("remote", 2 * seg + 2))
+        sides = [(T.lc[:, l:l + P2].bitcast(dt.uint8), T.sc[:, a:a + P2].bitcast(dt.uint8)), (T.ls[:, l:l + P2], T.ss[:, a:a + P2])]
+        if OPT["sfirst"]: sides.reverse()
+        for i, (dst, src) in enumerate(sides):
+            op("G", lambda dst=dst, src=src: g.remote_dma(dst, src, T.sem["arr%d" % seg], T.sem.sent, pid, rid, mask),
+               [("sc", seg)], [], ("remote", 2 * seg + 1 + i))
 
+    def tile_at(seg): return 4 * C + 4 * P2 * seg
     def tile_keys(seg): return [("tl", seg, b) for b in range(4)] if seg >= 0 else ["in_x"]
 
     def quant_piece(seg):
-        e = 4 * C + 4 * P2 * (seg + 1)
+        e = tile_at(seg + 1)
         qz(T.sc[:, 128 * seg:128 * seg + 128], T.ss[:, 128 * seg:128 * seg + 128], T.tl[:, e - 512:e],
            tile_keys(seg) + tile_keys(seg - 1), [("sc", seg)])
 
     def landed(seg):
         e = C + P2 * (seg + 1)
         return T.lc[:, e - 128:e], T.ls[:, e - 128:e], [("arr", seg), ("arr", seg - 1) if seg > 0 else ("qx", 0)]
+
+    def got(bank): return ps(bank)[:, 32:128]
 
     def qx(t, n=C):
         return (T.lc[:, 0:n], T.ls[:, 0:n]) if t == 0 else (T.qc[:, C * (t - 1):C * (t - 1) + n], T.qs[:, C * (t - 1):C * (t - 1) + n])
@@ -172,78 +185,87 @@ def rank_program(g, core, T, topo):
         return T.tl[:, b:4 * C:4] if t == 0 else T.xs[:, o + 4 * c0 + b:o + 4 * c1:4]
 
     def xkeys(t, parts=(0, 1)): return ["in_x"] if t == 0 else [("xs", t, b, c) for b in range(4) for c in parts]
+    def eb(b): return T.ec[:, 128 * b:128 * b + 128], T.es[:, 128 * b:128 * b + 128]
 
-    load("S", T.pli[:], "pl")
     load("A", T.ub[:], "u")
+    if OPT["plq"] == "S": load("S", T.pli[:], "pl")
     load("S", T.tl[:, 0:4 * C], "x")
+    if OPT["plq"] == "A": load("A", T.pli[:], "pl")
     load("S", T.w0c[:].bitcast(dt.uint8), "wc")
     load("S", T.w0s[:], "ws")
     load("S", T.w1c[:].bitcast(dt.uint8), "mc")
     load("S", T.w1s[:], "ms")
-    load("S", T.vb[:], "v")
 
-    iota(T.pi[:, 0:1], [[0, 1]], 0, 1, ["pi0"], small=False)
-    iota(T.pi[:, 1:2], [[0, 1]], 0, 2, ["pi1"], small=False)
-    iota(T.jj[:], [[1, 128]], 0, -1, ["jj"])
-    iota(T.io1[:, 0:8], [[32, 4], [0, 2]], 0, 0, ["io_u"])
-    iota(T.io1[:, 8:16], [[16, 8]], 2, 0, ["io_u2"])
-    iota(T.io1[:, 16:32], [[12, 2], [1, 4], [0, 2]], 0, 0, ["io_p"])
-    iota(T.io1[:, 32:44], [[16, 12]], 0, 0, ["io_n"])
-    iota(T.slot[:], [[0, 2], [1, P2]], 0, 0, ["slot"])
-    iota(T.cnt[:], [[1, C]], 0, 0, ["cnt"])
-
-    ms(T.ef[:], 0.0, ["ef"])
-    ms(T.ones[:], 1.0, ["ones"])
-    ms(T.dlt[:, 0:1], 0.0, [("dlt", 0)])
-    WT = [1, 2, 4, 8, 32, 64]
-    for col, src, m in ((0, 0, 1), (1, 0, 2), (2, 0, 4), (3, 0, 8), (8, 0, 15), (9, 0, 16), (4, 1, 32), (6, 1, 63), (7, 1, 48)):
-        ts(T.ai[:, col:col + 1], T.pi[:, src:src + 1], m, None, A.bitwise_and, None, ["pi%d" % src], [("ai", col)])
-    cp(T.af[:, 0:5], T.ai[:, 0:5], [("ai", c) for c in range(5)], ["af"])
-    cp(T.af[:, 6:10], T.ai[:, 6:10], [("ai", c) for c in range(6, 10)], ["af2"])
     af = lambda c: T.af[:, c:c + 1]
     tm = lambda c: T.tmp[:, c:c + 1]
+    iota(T.pi[:, 0:1], [[0, 1]], 0, 1, [("pi", 0)], small=False)
+    iota(T.pi[:, 1:2], [[0, 1]], 0, 16, [("pi", 1)], small=False)
+    iota(T.pi[:, 2:3], [[0, 1]], 63, 64, [("pi", 2)], small=False)
+    iota(T.jj[:], [[1, 128]], 0, -1, ["jj"])
+    iota(T.io1[:, 0:8], [[32, 4], [1, 2]], 0, 0, ["io_u"])
+    iota(T.io1[:, 8:16], [[16, 8]], 2, 0, ["io_u2"])
+    iota(T.io1[:, 32:40], [[-4, 2], [0, 4]], 2, 0, ["io_d0"])
+    iota(T.io1[:, 40:48], [[0, 2], [-2, 2], [0, 2]], 1, 0, ["io_d1"])
+    iota(T.io1[:, 16:32], [[0, 2], [1, 4], [0, 2]], 0, 0, ["io_p"])
+    iota(T.ones[:], [[0, 64]], -16, 0, ["ones"])
+    iota(T.io1[:, 48:56], [[128, 2], [16, 4]], 128, 0, ["io_s"])
+    iota(T.cnt[:], [[1, C]], 0, 0, ["cnt"])
+    iota(T.cn2[:], [[0, 2], [1, P2]], 0, 0, ["cn2"])
+    iota(T.tab[:, 256:384], [[0, 128]], 0, 0, ["tab3", "tab4"])
+    iota(T.pw2[:], [[0, 64]], 0, 0, [("pw", s) for s in range(1, 6)])
+    iota(T.bt[:], [[0, 32]], 0, 0, ["bt"])
+    for s in range(1, 6): iota(T.pw2[:, (1 << s) - 1:1 << s], [[0, 1]], -16, 0, [("pw", s)])
+    iota(T.xs[:, 0:XP], [[0, XP]], 0, 0, ["pad"])
+
+    ms(T.ef[:], 0.0, ["ef"])
+    BITS = [(0, 15), (0, 14), (0, 12), (0, 8), (0, 4), (0, 2), (0, 1), (0, 16), (1, 16), (2, 255)]
+    for col, (src, m) in enumerate(BITS):
+        ts(T.ai[:, col:col + 1], T.pi[:, src:src + 1], m, None, A.bitwise_and, None, [("pi", src)], [("ai", col)])
+    ms(T.dlt[:, 0:2], 0.0, [("dlt", 0)])
+    cp(T.af[:, 0:10], T.ai[:, 0:10], [("ai", c) for c in range(10)], ["af"])
+    ts(T.ef[:, 3:515:4], T.jj[:], 0.0, 0.5, A.is_equal, A.mult, ["jj", "ef"], ["ef"])
+    b0, row, b16 = af(6), af(0), af(7)
+
+    def qe(b): qz(*eb(b), T.ef[:, 3 - b:515 - b], ["ef"], [("e", b)])
+
+    WT = [1, 2, 4, 8, 32, 64]
+    dl = lambda a, b: T.dlt[:, 1 + a:1 + b]
 
     def double(s):
         w = 1 << s
         rd = [("dlt", i) for i in range(s + 1)]
-        if s < 5: ts(T.dlt[:, w:2 * w], T.dlt[:, 0:w], float(WT[s]), tm(40 + s), A.add, A.subtract, rd + ["a2"], [("dlt", s + 1)])
-        else: ts(T.dlt[:, w:2 * w], T.dlt[:, 0:w], float(WT[s]), None, A.add, None, rd, [("dlt", s + 1)])
+        if s < 4: ts(dl(w, 2 * w), dl(0, w), float(WT[s]), tm(43 - s), A.add, A.subtract, rd + ["a2"], [("dlt", s + 1)])
+        else: ts(dl(w, 2 * w), dl(0, w), float(WT[s]), None, A.add, None, rd, [("dlt", s + 1)])
 
-    def qe(b): qz(T.ec[:, 128 * b:128 * b + 128], T.es[:, 128 * b:128 * b + 128], T.ef[:, 3 - b:515 - b], ["ef"], [("e", b)])
+    lowat = lambda h: row if h == 4 else tm(h)
 
-    ts(T.tmp[:, 40:45], T.af[:, 0:5], 2.0, None, A.mult, None, ["af"], ["a2"])
-    cp(T.tmp[:, 8:13], T.af[:, 0:5], ["af"], ["dd"])
-    tt(tm(0), af(6), af(7), A.add, ["af2"], ["lo0"])
-    double(0)
-    ts(tm(11), af(3), 3.0, None, A.mult, None, ["af", "dd"], ["dd"])
-    double(1)
-    ts(T.ef[:, 3:515:4], T.jj[:], 0.0, None, A.is_equal, None, ["jj", "ef"], ["ef"])
-    scan(T.tmp[:, 1:6], T.ones[:, 0:5], T.tmp[:, 8:13], tm(0), A.mult, A.subtract, ["ones", "dd", "lo0"], ["lo1"])
-    double(2)
-    ts(tm(34), af(8), 2.0, 4.0, A.min, A.mult, ["af2"], ["t34"])
-    tt(T.tmp[:, 16:21], T.tmp[:, 40:45], T.tmp[:, 0:5], A.add, ["a2", "lo0", "lo1"], ["cc"])
-    double(3)
-    qe(0)
-    double(4)
-    qe(1)
-    double(5)
-    ts(T.prl[:], T.io1[:, 16:32], tm(34), None, A.add, None, ["io_p", "t34"], ["prl"])
-    aff(tm(32), af(2), 0.25, 0.0, ["af"], ["t32"])
-    aff(tm(35), af(0), 128.0, 63.0, ["af"], ["t35"])
-    aff(tm(33), af(0), 16.0, tm(32), ["af", "t32"], ["t33"])
-    aff(tm(36), af(1), 32.0, tm(35), ["af", "t35"], ["t36"])
-    cp(T.ul[:, 8:16], T.io1[:, 8:16], ["io_u2"], ["ul2"])
-    ts(T.ul[:, 0:8], T.io1[:, 0:8], tm(33), None, A.add, None, ["io_u", "t33"], ["ul"])
-    for h in range(6):
+    def low(h):
         a, w = (0, 2) if h == 0 else (1 << h, 2 << h)
-        aff(T.tab[:, a:w], T.ones[:, a:w], 0.0, tm(h), ["ones", "lo0", "lo1"], [("tab", 0, h)])
-    aff(tm(37), af(2), 64.0, tm(36), ["af", "t36"], ["cp"])
-    for h in range(6):
-        a, w = (0, 2) if h == 0 else (1 << h, 2 << h)
-        rd = [("dlt", i) for i in range(h + 2)] + ["cc", "lo1"]
-        if h < 3: aff(T.tab[:, 64 + a:64 + w], T.dlt[:, a:w], 1.0, tm(16 + h), rd, [("tab", 1, h)])
-        else: ts(T.tab[:, 64 + a:64 + w], T.dlt[:, a:w], tm(16 + h) if h < 5 else tm(5), None, A.add, None, rd, [("tab", 1, h)])
-    cp(T.plf[:], T.pli[:], ["in_pl"], ["plf"])
+        aff(T.tab[:, a:w], T.jj[:, a:w], 0.0, lowat(h), ["jj", "af", "lo", "lo5"], [("tab", 0, h)])
+
+    def high(h):
+        w = 1 << h
+        a = 0 if h else 1
+        ts(T.tab[:, 128 + w - a:128 + 2 * w], dl(-a, w), lowat(h), float(WT[h]), A.add, A.add,
+           [("dlt", i) for i in range(h + 1)] + ["af", "lo", "lo5"], [("tab", 1, h)])
+
+    tabs = [("tab", i, h) for i in range(2) for h in range(6)] + ["tab1", "tab2"]
+    consts = [
+        lambda: ts(T.tmp[:, 40:44], T.af[:, 3:7], 2.0, None, A.mult, None, ["af"], ["a2"]),
+        lambda: aff(tm(5), row, 1.0, 128.0, ["af"], ["lo5"]),
+        lambda: ts(T.tmp[:, 0:4], T.af[:, 0:4], row, tm(40), A.add, A.add, ["af", "a2"], ["lo"]),
+        lambda: ts(T.tab[:, 64:128], T.tab[:, 0:64], 16.0, None, A.add, None, tabs[0:6], ["tab1"]),
+        lambda: ts(T.tab[:, 192:256], T.tab[:, 128:192], 16.0, None, A.add, None, tabs[6:12], ["tab2"]),
+    ]
+    places = [
+        lambda: ts(tm(34), row, b0, 10.0, A.subtract, A.min, ["af"], ["t34"]),
+        lambda: ts(T.tmp[:, 48:64], T.io1[:, 32:48], b0, tm(34), A.mult, A.add, ["io_d0", "io_d1", "af", "t34"], ["p1"]),
+        lambda: tt(T.tmp[:, 64:80], T.tmp[:, 48:64], T.io1[:, 16:32], A.add, ["p1", "io_p"], ["p2"]),
+        lambda: ts(T.prl[:], T.tmp[:, 64:80], tm(34), None, A.add, None, ["p2", "t34"], ["prl"]),
+        lambda: cp(T.plf[:], T.pli[:], ["in_pl"], ["plf"]),
+        lambda: windows(0),
+        lambda: windows2(0),
+    ]
 
     def windows(t):
         acp(T.pre[:, 256 * t:256 * t + 256], T.plf[:, 24 * t:24 * t + 24].indirect(T.prl[:]), ["plf", "prl"], [("pre", t)])
@@ -251,237 +273,256 @@ def rank_program(g, core, T, topo):
     def windows2(t):
         tr(T.win[:, 256 * t:256 * t + 256], T.pre[:, 256 * t:256 * t + 256], [("pre", t)], [("win", t)])
 
-    tabs = [("tab", i, h) for i in range(2) for h in range(6)]
-    qe(2)
-    qe(3)
-    qz(T.uc[:], T.us[:], T.ub[:], ["in_u"], ["uq"])
-    aff(T.tab[:, 128:256], T.tab[:, 0:128], 1.0, 16.0, tabs, ["tab1"])
-    acp(T.ups[:, 0:128], T.us[:].indirect(T.ul[:, 0:8]), ["uq", "ul"], ["ups0"])
-    qz(T.lc[:, 0:C], T.ls[:, 0:C], T.tl[:, 0:4 * C], ["in_x"], [("qx", 0)])
-    cp(T.upc[:, 0:128].bitcast(dt.uint32), T.uc[:].bitcast(dt.uint32).indirect(T.ul[:, 0:8]), ["uq", "ul"], ["upc0"])
-    cp(T.upc[:, 128:256].bitcast(dt.uint32), T.uc[:].bitcast(dt.uint32).indirect(T.ul[:, 8:16]), ["uq", "ul2"], ["upc1"])
-    acp(T.ups[:, 128:256], T.us[:].indirect(T.ul[:, 8:16]), ["uq", "ul2"], ["ups1"])
-    windows(0)
-    aff(T.tab[:, 256:512], T.tab[:, 0:256], 1.0, 128.0, tabs + ["tab1"], ["tab2"])
-    ts(T.tmp[:, 48:50], T.io1[:, 32:34], af(8), 23.0, A.add, A.min, ["io_n", "af2"], ["nn"])
+    picks = [
+        lambda: ts(T.ul[:, 0:8], T.io1[:, 0:8], af(8), None, A.add, None, ["io_u", "af"], ["ul"]),
+        lambda: cp(T.ul[:, 8:16], T.io1[:, 8:16], ["io_u2"], ["ul2"]),
+        lambda: qz(T.uc[:], T.us[:], T.ub[:], ["in_u"], ["uq"]),
+        lambda: acp(T.ups[:, 0:128], T.us[:].indirect(T.ul[:, 0:8]), ["uq", "ul"], ["ups0"]),
+        lambda: cp(T.upc[:, 0:128].bitcast(dt.uint32), T.uc[:].bitcast(dt.uint32).indirect(T.ul[:, 0:8]), ["uq", "ul"], ["upc0"]),
+        lambda: acp(T.ups[:, 128:256], T.us[:].indirect(T.ul[:, 8:16]), ["uq", "ul2"], ["ups1"]),
+        lambda: cp(T.upc[:, 128:256].bitcast(dt.uint32), T.uc[:].bitcast(dt.uint32).indirect(T.ul[:, 8:16]), ["uq", "ul2"], ["upc1"]),
+        lambda: qz(*qx(0), T.tl[:, 0:4 * C], ["in_x"], [("qx", 0)]),
+    ]
 
-    def direction(t, bank, c0):
+    def direction(t, p0=0):
         mx, lt, st = T.mxv[:, t:t + 1], T.ltv[:, 64 * t:64 * t + 63], T.stv[:, 64 * t:64 * t + 63]
         last = T.stv[:, 64 * t + 62:64 * t + 63]
-        s = ps(bank)[:, c0 + 1:c0 + 64]
-        return [
-            lambda: op("V", lambda: vec.tensor_reduce(mx, s, AxisListType.X, A.max), [("ps", bank)], [("mx", t)]),
-            lambda: ts(lt, s, mx, -1000.0, A.is_lt, A.mult, [("ps", bank), ("mx", t)], [("lt", t)]),
-            lambda: scan(st, T.ones[:, 0:63], lt, -1000.0, A.add, A.max, ["ones", ("lt", t)], [("st", t)]),
-            lambda: ts(T.of0[:, 2 * t:2 * t + 1], last, -1.0, tm(37), A.mult, A.add, [("st", t), "cp"], [("of0", t)]),
-            lambda: (cp(T.g0[:, 16 * t:16 * t + 16], T.tab[:].indirect(T.of0[:, 2 * t:2 * t + 1]), tabs + ["tab1", "tab2", ("of0", t)], [("g0", t)]),
-                     acp(T.g1[:, 128 * t:128 * t + 128], T.win[:, 256 * t:256 * t + 256].indirect(T.g0[:, 16 * t:16 * t + 8]),
-                         [("win", t), ("g0", t)], [("g1", t)])),
-            lambda: tr(T.g1t[:, 128 * t:128 * t + 128], T.g1[:, 128 * t:128 * t + 128], [("g1", t)], [("g1t", t)]),
-            lambda: cp(T.fw[:, 32 * t:32 * t + 32], T.g1t[:, 128 * t:128 * t + 128].indirect(T.fnl[:, 0:2]),
-                       [("g1t", t), ("fnl", 0), ("fnl", 1)], [("fw", t)]),
+        s = ps(0)[:, p0 + 1:p0 + 64]
+        of = T.of0[:, 2 * t:2 * t + 1]
+        head = [
+            lambda: op("V", lambda: vec.tensor_reduce(mx, s, AxisListType.X, A.max), [("ps", 0)], [("mx", t)]),
+            lambda: ts(lt, s, mx, 16000.0, A.is_lt, A.mult, [("ps", 0), ("mx", t)], [("lt", t)]),
+            lambda: scan(st, T.ones[:, 0:63], lt, 16000.0, A.add, A.min, ["ones", ("lt", t)], [("st", t)]),
+        ]
+        if t > 0:
+            top = T.stw[:, 64 * t:64 * t + 63]
+            return head + [
+                lambda: scan(top, T.pw2[:, 0:63], lt, 16000.0, A.add, A.min, [("pw", s) for s in range(1, 6)] + [("lt", t)], [("sw", t)]),
+                lambda: ts(of, last, tm(57), None, A.add, None, [("st", t), "chi"], [("of0", t)]),
+                lambda: ts(T.of0[:, 2 * t + 1:2 * t + 2], T.stw[:, 64 * t + 62:64 * t + 63], tm(58), None, A.add, None, [("sw", t), "clo"], [("of1", t)]),
+                lambda: cp(T.fw[:, 64 * t:64 * t + 32], T.bigt[:].indirect(T.of0[:, 2 * t:2 * t + 2]),
+                           [("bigt", 0), ("bigt", 1), ("of0", t), ("of1", t)], [("fw", t)]),
+            ]
+        return head + [
+            lambda: ts(of, last, 1.0 / 16.0, af(9), A.mult, A.add, [("st", t), "af"], [("of0", t)]),
+            lambda: cp(T.g0[:, 16 * t:16 * t + 16], T.tab[:, 0:256].indirect(of), tabs + [("of0", t)], [("g0", t)]),
+            lambda: cp(T.g1[:, 64 * t:64 * t + 64], T.win[:, 256 * t:256 * t + 256].indirect(T.g0[:, 16 * t:16 * t + 4]),
+                       [("win", t), ("g0", t)], [("g1", t)]),
+            lambda: tr(T.g1t[:, 64 * t:64 * t + 64], T.g1[:, 64 * t:64 * t + 64], [("g1", t)], [("g1t", t)]),
+            lambda: cp(T.fw[:, 64 * t:64 * t + 64], T.g1t[:, 64 * t:64 * t + 64], [("g1t", t)], [("fw", t)]),
         ]
 
-    rest = []
+    def sign(t, part, bank, c0, c1, p0):
+        op("A", lambda: act.activation(T.sg[:, C * t + c0:C * t + c1], ps(bank)[:, p0:p0 + c1 - c0], SG, bias=-TINY), [("ps", bank)], [("sg", t, c) for c in part])
+
+    def vmul(t, b, part, bank, c0, c1, p0):
+        a = 4 * C * t + C * b
+        tt(T.vv[:, a + c0:a + c1], ps(bank)[:, p0:p0 + c1 - c0], T.sg[:, C * t + c0:C * t + c1], A.mult,
+           [("ps", bank)] + [("sg", t, c) for c in part], [("vv", t, b, c) for c in part])
+
+    def products(t, n, everything=True):
+        xa, xn, kq = qx(t, 128), qx(t, n), [("qx", t)]
+        if t == 0 and everything: mm(ps(0)[:, 0:128], T.upc[:, 0:128], T.ups[:, 0:128], *xa, kq + ["upc0", "ups0"], [("ps", 0)])
+        else: mm(ps(0)[:, 0:128], T.upc[:, 256:384], T.ups[:, 256:384], *xa, kq + ["upc2", "ups2"], [("ps", 0)])
+        if not everything: return
+        mm(ps(1)[:, 0:n], T.upc[:, 128:256], T.ups[:, 128:256], *xn, kq + ["upc1", "ups1"], [("ps", 1)])
+        for b in range(4):
+            mm(ps(2 + b)[:, 0:n], *eb(b), *xn, kq + [("e", b)], [("ps", 2 + b)])
+
+    d = direction(0)
+    steps = {"c": lambda i: consts[i](), "p": lambda i: places[i](), "u": lambda i: picks[i](), "e": qe, "x": double, "l": low, "h": high,
+             "m": lambda i: products(0, C), "s": lambda i: sign(0, (0, 1), 1, 0, C, 0), "d": lambda i: d[i](),
+             "v": lambda b: vmul(0, b, (0, 1), 2 + b, 0, C, 0)}
+    for s in OPT["start"].split(): steps[s[0]](int(s[1]))
+
     for t in range(R):
         lender = T.cores[(rank + 1 + t) % n_ranks]
         borrower = T.cores[(rank - 1 - t) % n_ranks]
-        xc, xsc = qx(t)
-        o4, s0 = 4 * C * t, 4 * t
-        kq = [("qx", t)]
-        late = t == 0 or not OPT["early"]
-        if late:
-            xa = qx(t, 128)
-            mm(ps(0)[:, 0:128], T.upc[:, 0:128], T.ups[:, 0:128], xa[0], xa[1], kq + ["upc0", "ups0"], [("ps", 0)])
-            d = direction(t, 0, 0)
-        mm(ps(1)[:, 0:C], T.upc[:, 128:256], T.ups[:, 128:256], xc, xsc, kq + ["upc1", "ups1"], [("ps", 1)])
-        for b in range(4):
-            mm(ps(2 + b)[:, 0:C], T.ec[:, 128 * b:128 * b + 128], T.es[:, 128 * b:128 * b + 128], xc, xsc, kq + [("e", b)], [("ps", 2 + b)])
-        sgn = T.sg[:, C * t:C * t + C]
-
-        def sign(): ts(sgn, ps(1)[:, 0:C], 0.0, 0.5, A.is_gt, A.subtract, [("ps", 1)], [("sg", t)])
-
-        def vmul(b):
-            tt(T.vv[:, o4 + C * b:o4 + C * b + C], ps(2 + b)[:, 0:C], sgn, A.mult, [("ps", 2 + b), ("sg", t)], [("vv", t, b)])
+        o4, o8, s0 = 4 * C * t, 4 * W2 * t, 4 * t
+        fwa = lambda k, side, t=t: 64 * t + (32 * side + 22 * k if t == 0 else 16 * (1 - side) + 6 * k)
+        fwl = lambda k, side: T.fw[:, fwa(k, side):fwa(k, side) + 6]
+        fyl = lambda k, t=t: T.fy[:, 24 * t + 12 * k:24 * t + 12 * k + 12]
+        fyk = lambda k, t=t: [("fy", t, k, 0), ("fy", t, k, 1)]
 
         def pair(k, b):
-            z0 = 4 * C + 4 * P2 * (s0 + k)
+            z0 = tile_at(s0 + k)
             w = T.vv[:, o4 + C * b:o4 + C * b + C]
             l = T.lo[:, o4 + 4 * P2 * k + P2 * b:o4 + 4 * P2 * k + P2 * b + P2]
-            f = 32 * t + 12 * k
-            return (lambda: acp(l, w.indirect(T.fw[:, f:f + 6]), [("vv", t, b), ("fw", t)], [("lo", t, k, b)]),
-                    lambda: tt(T.tl[:, z0 + b:z0 + 4 * P2:4], w.indirect(T.fw[:, f + 6:f + 12]), l, A.add,
-                               [("vv", t, b), ("fw", t), ("lo", t, k, b)], [("tl", s0 + k, b)]))
+            vk = [("vv", t, b, 0), ("vv", t, b, 1), ("fw", t)]
+            (cp if OPT["vlo"] and k == 0 and b == 0 else acp)(l, w.indirect(fwl(k, 0)), vk, [("lo", t, k, b)])
+            tt(T.tl[:, z0 + b:z0 + 4 * P2:4], w.indirect(fwl(k, 1)), l, A.add, vk + [("lo", t, k, b)], [("tl", s0 + k, b)])
 
-        if late:
-            if t == 0: ts(T.tmp[:, 50:52], T.tmp[:, 48:50], 1.0 / 3.0, 1.0 / 3.0, A.mult, A.subtract, ["nn"], ["n3"])
-            d[0]()
-            if t == 0: cp(T.tmi[:, 0:2], T.tmp[:, 50:52], ["n3"], ["n3i"])
-            d[1]()
-            sign()
-            d[2]()
-            vmul(0)
-            d[3]()
-            vmul(1)
-            if t == 0: windows2(0)
-            d[4]()
-            vmul(2)
-            if t == 0:
-                for c in range(2):
-                    ts(T.fnl[:, c:c + 1], T.tmi[:, c:c + 1], 13.0, tm(48 + c), A.mult, A.add, ["n3i", "nn"], [("fnl", c)])
-            d[5]()
-            vmul(3)
-            d[6]()
-            for b in range(4):
-                for f in pair(0, b): f()
-        else:
-            rest[0]()
-            sign()
-            vmul(0)
-            rest[1]()
-            vmul(1)
-            rest[2]()
-            pr = [pair(0, b) for b in range(4)]
-            pr[0][0]()
-            pr[1][0]()
-            vmul(2)
-            vmul(3)
-            pr[2][0]()
-            pr[3][0]()
-            for b in range(4): pr[b][1]()
-        quant_piece(s0)
-        send(s0, lender, borrower)
-        for b in range(4):
-            for f in pair(1, b): f()
-        quant_piece(s0 + 1)
-        send(s0 + 1, lender, borrower)
+        yw = lambda b, c0=0, c1=C: T.yh[:, o4 + C * b + c0:o4 + C * b + c1]
+        sgh = T.sh[:, C * t:C * t + C]
 
         def ymul(b):
-            tt(T.yh[:, o4 + C * b:o4 + C * b + C], xcol(t, b), sgn, A.mult, xkeys(t) + [("sg", t)], [("yh", t, b)])
+            tt(yw(b), xcol(t, b), sgh, A.mult, xkeys(t) + [("sh", t)], [("yh", t, b)])
 
         def yperm(b):
             a = o4 + C * b
-            acp(T.yp[:, a:a + C], T.yh[:, a:a + C].indirect(T.fw[:, 32 * t:32 * t + 12]), [("yh", t, b), ("fw", t)], [("yp", t, b)])
+            acp(T.yp[:, a:a + C], yw(b).indirect(fyl(0)), [("yh", t, b)] + fyk(0), [("yp", t, b)])
+
+        for k in range(2):
+            for b in range(4): pair(k, b)
+            quant_piece(s0 + k)
+            send(s0 + k, lender, borrower)
 
         def lend(k):
             rc, rs, keys = landed(s0 + k)
             wc_, ws_, wk = (T.w0c, T.w0s, ["in_wc", "in_ws"]) if k == 0 else (T.w1c, T.w1s, ["in_mc", "in_ms"])
-            h0 = 4 * C + 4 * P2 * (s0 + 2 + k)
+            h0 = tile_at(s0 + 2 + k)
             for b in range(4):
                 mm(ps(4 * k + b)[:, 0:128], wc_[:, 128 * b:128 * b + 128], ws_[:, 128 * b:128 * b + 128], rc, rs, keys + wk, [("ps", 4 * k + b)])
             for b in range(4):
-                o, i = T.tl[:, h0 + b:h0 + 4 * P2:4], ps(4 * k + b)[:, 32:128]
-                if b % 2 == 0: asc(o, i, 0.03125, [("ps", 4 * k + b)], [("tl", s0 + 2 + k, b)])
+                o, i = T.tl[:, h0 + b:h0 + 4 * P2:4], got(4 * k + b)
+                if b in OPT["aev"]: asc(o, i, 0.03125, [("ps", 4 * k + b)], [("tl", s0 + 2 + k, b)])
                 else: ts(o, i, 0.03125, None, A.mult, None, [("ps", 4 * k + b)], [("tl", s0 + 2 + k, b)])
             quant_piece(s0 + 2 + k)
             send(s0 + 2 + k, borrower, lender)
 
-        n0 = 768 * t
-        if t == 0:
-            aff(tm(52), af(9), 1.0 / 16.0, 0.0, ["af2"], ["m1"])
-            aff(tm(53), af(9), -1.0 / 16.0, 1.0, ["af2"], ["m0"])
-            aff(tm(54), af(9), C / 16.0, 0.0, ["af2"], ["c0"])
-            aff(tm(55), af(9), -C / 16.0, float(C), ["af2"], ["c1"])
-        if t + 1 < R: windows(t + 1)
-        for b in range(4): ymul(b)
-        yperm(0)
-        yperm(1)
-        if t == 0:
-            ms(T.inv0[:], 0.0, ["z0", "inv0"])
-            ms(T.inv1[:], 0.0, ["z1", "inv1"])
-            ms(T.bt[:], 0.0, ["bt"])
-            ts(T.tmp[:, 20:32], T.io1[:, 32:44], af(8), None, A.add, None, ["io_n", "af2"], ["cc"])
-            ts(T.hf[:], T.ef[:], 0.5, None, A.mult, None, ["ef"], ["hf"])
+        def table(i):
+            if t + 1 == R: return
+            a, e = (0, HALF) if i == 0 else (HALF, BIG)
+            acp(T.big[:, a:e], T.win[:, 256 * (t + 1):256 * (t + 2)].indirect(T.bgl[:, a // 16:e // 16]), [("win", t + 1), "bgl"], [("big", i)])
+
+        def table2(i):
+            if t + 1 == R: return
+            a, e = (0, HALF) if i == 0 else (HALF, BIG)
+            tr(T.bigt[:, a:e], T.big[:, a:e], [("big", i)], [("bigt", i)])
+
+        def compact(k):
             for e in range(2):
-                ts(T.stl[:, e:24:2], T.tmp[:, 20:32], tm(53 - e), tm(54 + e), A.mult, A.add, ["cc", "m0", "m1", "c0", "c1"], [("stl", e)])
-            for b in range(4):
-                qz(T.hc[:, 128 * b:128 * b + 128], T.hs[:, 128 * b:128 * b + 128], T.hf[:, 3 - b:515 - b], ["hf"], [("h", b)])
-        for e in range(2):
-            ts(T.fd[:, 24 * t + e:24 * t + 24:2], T.fw[:, 32 * t:32 * t + 12], tm(53 - e), tm(54 + e), A.mult, A.add,
-               [("fw", t), "m0", "m1", "c0", "c1"], [("fd", t, e)])
-        ts(T.bt[:, t:t + 1], T.stv[:, 64 * t + 62:64 * t + 63], -1.0, 63.0, A.mult, A.add, [("st", t), "bt"], [("btc", t)])
-        if t + 1 < R: windows2(t + 1)
-        lend(0)
-        yperm(2)
-        cp(T.inv1[:, 0:C].indirect(T.fw[:, 32 * t + 12:32 * t + 24]), T.slot[:], ["slot", ("fw", t)], ["inv1"])
-        lend(1)
-        yperm(3)
-        acp(T.nw[:, n0 + 384:n0 + 768], T.inv1[:].indirect(T.fd[:, 24 * t:24 * t + 24]), ["inv1", "z1", ("fd", t, 0), ("fd", t, 1)], [("nw", t, 1)])
-        cp(T.inv0[:, 0:C].indirect(T.fw[:, 32 * t:32 * t + 12]), T.cnt[:], ["cnt", ("fw", t)], ["inv0"])
-        acp(T.nw[:, n0:n0 + 384], T.inv0[:].indirect(T.stl[:]), ["inv0", "z0", ("stl", 0), ("stl", 1)], [("nw", t, 0)])
+                cp(T.fy[:, 24 * t + 12 * k + 6 * e:24 * t + 12 * k + 6 * e + 6], fwl(k, e), [("fw", t)], [("fy", t, k, e)])
+
+        again = direction(R)
+        once = [
+            lambda: (aff(tm(52), b16, 1.0 / 16.0, 0.0, ["af"], ["par"]), aff(tm(59), b0, 64.0, af(1), ["af"], ["w59"]),
+                     aff(tm(4), row, 1.0, 0.0, ["af"], ["lo4"]), ts(tm(60), row, 6.0, None, A.is_ge, None, ["af"], ["w60"])),
+            lambda: (ts(T.ul[:, 16:24], T.io1[:, 8:16], tm(60), -2.0, A.add, A.add, ["io_u2", "w60"], ["ul3"]),
+                     ts(T.sl[:], T.io1[:, 48:56], tm(59), tm(52), A.add, A.add, ["io_s", "w59", "par"], ["sl"]),
+                     cp(T.tab[:, 256:262], T.tmp[:, 0:6], ["lo", "lo4", "lo5"], ["tab3"]),
+                     ts(T.tab[:, 320:326], T.tmp[:, 0:6], 16.0, None, A.add, None, ["lo", "lo4", "lo5"], ["tab4"])),
+            lambda: cp(T.bgl[:], T.tab[:].indirect(T.sl[:, 0:5]), tabs + ["sl", "tab3", "tab4"], ["bgl"]),
+            lambda: (acp(T.ups[:, 256:384], T.us[:].indirect(T.ul[:, 16:24]), ["uq", "ul3"], ["ups2"]),
+                     cp(T.upc[:, 256:384].bitcast(dt.uint32), T.uc[:].bitcast(dt.uint32).indirect(T.ul[:, 16:24]), ["uq", "ul3"], ["upc2"]),
+                     products(0, 128, False)),
+            lambda: (ms(T.iv[:], 0.0, ["inv0", "nw"]), ts(tm(53), b0, 32.0, 384.0, A.mult, A.add, ["af"], ["w53"])),
+            lambda: (ts(tm(54), row, b0, 16.0, A.subtract, A.mult, ["af"], ["w54"]),
+                     ts(tm(56), b0, tm(52), tm(53), A.not_equal, A.mult, ["af", "par", "w53"], ["w56"])),
+            lambda: ts(tm(55), tm(56), tm(54), b16, A.add, A.add, ["af", "w54", "w56"], ["w55"]),
+            lambda: ts(T.gl[:, 0:1], tm(55), 607.0, None, A.min, None, ["w55"], ["gl"]),
+            lambda: ms(T.ad[:, 0:4 * W2:2], LOW, ["ad0"]),
+            lambda: (aff(tm(57), row, 1.0, 1008.0, ["af"], ["chi"]), aff(tm(58), row, 1.0, 1104.0, ["af"], ["clo"])),
+        ]
+
+        def invert(k):
+            if k: cp(T.inv1[:].indirect(fyl(1)), T.cn2[:], ["cn2"] + fyk(1), ["inv1"])
+            else: cp(T.iv[:, 16:16 + C].indirect(fyl(0)), T.cnt[:], ["cnt"] + fyk(0), ["inv0"])
+
+        def turn(i):
+            if i: tr(T.ivt[:, 384:800], T.iv[:], ["inv0", "nw"], ["ivB"])
+            else: tr(T.ivt[:, 0:384], T.iv[:, 16:400], ["inv0", "nw"], ["ivA"])
 
         def lists(k):
-            a = n0 + 384 * k
-            return [lambda: tr(T.ntr[:, a:a + 384], T.nw[:, a:a + 384], [("nw", t, k)], [("ntr", t, k)]),
-                    lambda: tt(T.n24[:, 32 * t + 12 * k:32 * t + 12 * k + 12], T.ntr[:, a:a + 384:32], T.ntr[:, a + 16:a + 384:32], A.add,
-                               [("ntr", t, k)], [("n24", t, k)])]
+            a = 32 * t + 16 * (1 - k)
+            if k: cp(T.bl[:, a:a + 16], T.ivt[:, C:800].indirect(T.gl[:, 0:1]), ["ivA", "ivB", "gl"], [("bl", t, 1)])
+            else: ts(T.bl[:, a:a + 16], T.ivt[:].indirect(T.gl[:, 0:1]), 2.0, 1.0, A.mult, A.add, ["ivA", "ivB", "gl"], [("bl", t, 0)])
 
-        l0, l1 = lists(0), lists(1)
-        l1[0]()
-        if t == 0:
-            ms(T.xs[:, 0:XP], 0.0, [("xs", 0, b, 1) for b in range(4)])
-            qz(T.vc[:], T.vs[:], T.vb[:], ["in_v"], ["vq"])
-        l1[1]()
-        for e in range(2):
-            a = 48 * t + 12 * e
-            ts(T.bl[:, a:a + 12], T.n24[:, 32 * t + 12:32 * t + 24], float(P2 * e), None, A.add, None, [("n24", t, 1)], [("bl", t, e)])
-        l0[0]()
-        if t == R - 1:
-            tr(T.btt[:], T.bt[:], ["bt"] + [("btc", i) for i in range(R)], ["btt"])
-        l0[1]()
-        if t == R - 1:
-            for k in range(2):
-                cp(T.odt[:, k:4:2], T.btt[:, 4 * k:4 * k + 2], ["btt"], [("odt", k)])
-            for gr in range(8):
-                store("S", T.od[gr:gr + 1, :], T.odt[32 * (gr // 2):32 * (gr // 2) + R, 2 * (gr % 2):2 * (gr % 2) + 2], [("odt", 0), ("odt", 1)])
-        cp(T.bl[:, 48 * t + 24:48 * t + 36], T.n24[:, 32 * t:32 * t + 12], [("n24", t, 0)], [("bl", t, 2)])
+        def note(i):
+            c = t if t else R
+            aff(T.bt[:, t:t + 1], T.stv[:, 64 * c + 62:64 * c + 63], 1.0 / 16.0, 63.0, [("st", c), "bt"], [("btc", t)])
+
+        def directions(i):
+            if i == 0: tr(T.btt[:], T.bt[:], ["bt"] + [("btc", j) for j in range(R)], ["btt"])
+            if i == 1:
+                for k in range(2):
+                    cp(T.odt[:, k:4:2], T.btt[:, 6 * k:32:16], ["btt"], [("odt", k)])
+                for gr in range(8):
+                    store("S", T.od[gr:gr + 1, :], T.odt[32 * (gr // 2):32 * (gr // 2) + R, 2 * (gr % 2):2 * (gr % 2) + 2], [("odt", 0), ("odt", 1)])
+
+        if t == 0: load("S", T.vb[:], "v", [("sc", 1)])
+        steps = {"c": compact, "i": invert, "y": ymul, "p": yperm, "t": table, "T": table2, "r": turn, "l": lists, "b": note, "L": lend,
+                 "s": lambda i: ts(sgh, T.sg[:, C * t:C * t + C], 0.5, None, A.mult, None, [("sg", t, 0), ("sg", t, 1)], [("sh", t)]),
+                 "n": lambda i: acp(T.iv[:, 208:208 + C], T.inv1[:].indirect(fyl(0)), ["inv1"] + fyk(0), ["nw"]),
+                 "w": windows, "W": windows2, "k": lambda i: once[i](), "a": lambda i: again[i](), "d": directions,
+                 "v": lambda i: qz(T.vc[:], T.vs[:], T.vb[:], ["in_v"], ["vq"])}
+        for s in OPT["wait"][t].split(): steps[s[0]](int(s[1]))
+        l1 = T.bl[:, 32 * t:32 * t + 12]
         for k in range(2):
             rc, rs, keys = landed(s0 + 2 + k)
             for b in range(4):
-                mm(ps(4 * k + b)[:, 0:128], T.hc[:, 128 * b:128 * b + 128], T.hs[:, 128 * b:128 * b + 128], rc, rs, keys + [("h", b)], [("ps", 4 * k + b)])
-        for b in range(4):
-            a = 4 * P2 * t + P2 * b
-            acp(T.dh[:, a:a + P2], ps(4 + b)[:, 32:128], [("ps", 4 + b)], [("dh", t, b)])
-        for b in range(4):
+                mm(ps(4 * k + b)[:, 0:128], *eb(b), rc, rs, keys + [("e", b)], [("ps", 4 * k + b)])
+        dh = lambda b: T.dh[:, 4 * P2 * t + P2 * b:4 * P2 * t + P2 * (b + 1)]
+
+        def bring(b):
+            acp(T.ad[:, W2 * b + 1:W2 * (b + 1):2], dh(b).indirect(l1), [("dh", t, b), ("bl", t, 1), "ad0"], [("ad", b)])
+
+        def order(b):
             for e in range(2):
-                a = o4 + C * b + P2 * e
-                tt(T.qq[:, a:a + P2], ps(b)[:, 32:128], T.yp[:, a:a + P2], A.max, [("ps", b), ("yp", t, b)], [("qq", t, b, e)])
-                tt(T.pp[:, a:a + P2], ps(b)[:, 32:128], T.yp[:, a:a + P2], A.min, [("ps", b), ("yp", t, b)], [("pp", t, b, e)])
-        half = lambda buf, c: buf[:, o4 + 2 * C * c:o4 + 2 * C * (c + 1)]
-        both = lambda n, c: [(n, t, 2 * c + i, e) for i in range(2) for e in range(2)]
-        for c in range(2):
-            a = 4 * P2 * t + 2 * P2 * c
-            tt(half(T.rr, c), T.dh[:, a:a + 2 * P2].indirect(T.bl[:, 48 * t:48 * t + 24]), half(T.qq, c), A.min,
-               [("dh", t, 2 * c), ("dh", t, 2 * c + 1), ("bl", t, 0), ("bl", t, 1)] + both("qq", c), [("rr", t, c)])
-        for c in range(2):
-            tt(half(T.mm, c), half(T.pp, c), half(T.rr, c), A.max, both("pp", c) + [("rr", t, c)], [("mm", t, c)])
+                a, y = o8 + W2 * b + C * e, T.yp[:, o4 + C * b + P2 * e:o4 + C * b + P2 * (e + 1)]
+                tt(T.pq[:, a:a + C:2], got(b), y, A.max, [("ps", b), ("yp", t, b)], [("pq", t, b, e, 0)])
+                tt(T.pq[:, a + 1:a + C:2], got(b), y, A.min, [("ps", b), ("yp", t, b)], [("pq", t, b, e, 1)])
+
+        def fetch(b): (acp if b < OPT["adh"] else cp)(dh(b), got(4 + b), [("ps", 4 + b)], [("dh", t, b)])
+
+        def middle(b):
+            a = o8 + W2 * b
+            scan(T.mo[:, a:a + W2], T.ad[:, W2 * b:W2 * (b + 1)], T.pq[:, a:a + W2], 0.0, A.min, A.max,
+                 [("ad", b), "ad0"] + [("pq", t, b, e, i) for e in range(2) for i in range(2)], [("mo", t, b)])
+
+        regained = {}
+
+        def regain(b, c0):
+            if t + 1 == R and c0: return
+            a, l = o8 + W2 * b, 32 * t + 16
+            acp(T.mc2[:, C * b + c0:C * b + C], T.mo[:, a:a + W2].indirect(T.bl[:, l + c0 // 16:l + C // 16]), [("mo", t, b), ("bl", t, 0)], [("mc2", b)])
+            regained[b] = c0
 
         def add(b, c0, c1, parts):
-            a, l = o4 + C * b, 48 * t + 24
-            tt(xcol(t + 1, b, c0, c1), T.mm[:, a:a + C].indirect(T.bl[:, l + c0 // 16:l + c1 // 16]), T.yh[:, a + c0:a + c1], A.add,
-               [("mm", t, b // 2), ("yh", t, b), ("bl", t, 2)], [("xs", t + 1, b, c) for c in parts])
+            a, l = o8 + W2 * b, 32 * t + 16
+            if c0 >= regained.get(b, C):
+                tt(xcol(t + 1, b, c0, c1), T.mc2[:, C * b + c0:C * b + c1], yw(b, c0, c1), A.add, [("mc2", b), ("yh", t, b)], [("xs", t + 1, b, c) for c in parts])
+                return
+            tt(xcol(t + 1, b, c0, c1), T.mo[:, a:a + W2].indirect(T.bl[:, l + c0 // 16:l + c1 // 16]), yw(b, c0, c1), A.add,
+               [("mo", t, b), ("yh", t, b), ("bl", t, 0)], [("xs", t + 1, b, c) for c in parts])
 
-        if OPT["early"] and t + 1 < R:
-            for b in range(4): add(b, 0, 64, (0,))
-            e = XP + o4 + 256
-            qz(T.dc[:, 128 * t:128 * t + 128], T.ds[:, 128 * t:128 * t + 128], T.xs[:, e - 512:e],
-               xkeys(t + 1, (0,)) + [("xs", t, b, 1) for b in range(4)], [("dq", t)])
-            mm(ps(0)[:, 0:128], T.upc[:, 0:128], T.ups[:, 0:128], T.dc[:, 128 * t:128 * t + 128], T.ds[:, 128 * t:128 * t + 128],
-               [("dq", t), "upc0", "ups0"], [("ps", 0)])
-            d = direction(t + 1, 0, 64)
-            add(0, 64, C, (1,))
-            d[0]()
-            add(1, 64, C, (1,))
-            d[1]()
-            add(2, 64, C, (1,))
-            d[2]()
-            add(3, 64, C, (1,))
-            d[3]()
-            rest = d[4:]
+        whole = t + 1 == R
+        ca, u, x0 = OPT["ca"], t + 1, XP + o4
+        head = lambda b: add(b, 0, C, (0, 1)) if whole or ca == C else add(b, 0, ca, (0,))
+        steps = {"o": order, "f": fetch, "b": bring, "m": middle, "h": head, "g": lambda b: regain(b, ca), "G": lambda b: regain(b, 0)}
+        for s in OPT["back"].split(): steps[s[0]](int(s[1]))
+        if whole or ca == C:
+            qz(*qx(u), T.xs[:, x0:x0 + 4 * C], xkeys(u), [("qx", u)])
+            if not whole:
+                products(u, C)
+                d = direction(u)
+                steps = {"d": lambda i: d[i](), "s": lambda i: sign(u, (0, 1), 1, 0, C, 0), "w": lambda b: vmul(u, b, (0, 1), 2 + b, 0, C, 0)}
+                for s in OPT["seq"].split(): steps[s[0]](int(s[1]))
         else:
-            for b in range(4): add(b, 0, C, (0, 1))
-        nc, ns = qx(t + 1)
-        qz(nc, ns, T.xs[:, XP + o4:XP + o4 + 4 * C], xkeys(t + 1), [("qx", t + 1)])
+            if OPT["afill"]: add(0, ca, C, (1,))
+            pa = 128 - ca
+            qz(*qx(u, 128), T.xs[:, x0 + 4 * ca - 512:x0 + 4 * ca], xkeys(u, (0,)) + (xkeys(t, (1,)) + ["pad"] if pa else []), [("qx", u)])
+            nb = C if OPT["ball"] else 128
+            products(u, 128, not OPT["ball"])
+            d = direction(u, pa)
+            bc, bs = T.dc[:, C * t:C * t + nb], T.ds[:, C * t:C * t + nb]
+            banks = (2, 3, 4, 5) if OPT["ball"] else (7, 1, 0, 2)
+            cb = 0 if OPT["ball"] else ca
+            pb, kb = cb - (C - nb), ((0, 1) if OPT["ball"] else (1,))
+
+            def rest():
+                qz(bc, bs, T.xs[:, x0 + 4 * (C - nb):x0 + 4 * C], xkeys(u), [("qb", u)])
+                mm(ps(6)[:, 0:nb], T.upc[:, 128:256], T.ups[:, 128:256], bc, bs, [("qb", u), "upc1", "ups1"], [("ps", 6)])
+                for b in range(4 if OPT["ball"] else 3): mm(ps(banks[b])[:, 0:nb], *eb(b), bc, bs, [("qb", u), ("e", b)], [("ps", banks[b])])
+                sign(u, kb, 6, cb, C, pb)
+
+            def first(b):
+                vmul(u, b, (0,), 2 + b, 0, ca, pa)
+                if b == 0: mm(ps(2)[:, 0:128], *eb(3), bc, bs, [("qb", u), ("e", 3)], [("ps", 2)])
+
+            steps = {"a": lambda b: add(b, ca, C, (1,)), "d": lambda i: d[i](), "q": lambda i: rest(), "s": lambda i: sign(u, (0,), 1, 0, ca, pa),
+                     "v": first, "w": lambda b: vmul(u, b, kb, banks[b], cb, C, pb)}
+            for s in OPT["seq"].split(): steps[s[0]](int(s[1]))
 
     xc, xsc = qx(R)
     kq = [("qx", R)]
@@ -489,7 +530,7 @@ def rank_program(g, core, T, topo):
     store("S", T.oc[:, :], xc.bitcast(dt.uint8), kq)
     c0 = C * (R - 1)
     for i in range(4):
-        store("A" if i == 3 else "S", T.osc[4 * i:4 * i + 4, :], T.qs[32 * i:32 * i + 4, c0:c0 + C], kq)
+        store("ASSS"[i], T.osc[4 * i:4 * i + 4, :], T.qs[32 * i:32 * i + 4, c0:c0 + C], kq)
     cp(T.yo[:], ps(0)[:, 0:C], [("ps", 0)], ["yo"])
     store("A", T.y[:, :], T.yo[:], ["yo"])
     emit(ops, queues, T, [("sent", sent[0]), ("st", stores[0])], landing)

@@ -8,14 +8,14 @@ XP = 256
 BIG, HALF = 16 * (64 + 6), 576
 LOW = -1.0e29
 TINY = 2.0 ** -120
-OPT = {"aev": (), "adh": 1, "vlo": False, "pre": 3, "sfirst": False, "ash": False, "plq": "S", "ca": 64, "ball": False, "afill": True,
-       "start": "c0 c1 e0 c2 x0 p0 x1 u0 x2 e1 x3 u1 x4 p1 e2 p2 e3 p3 l0 l1 l2 l3 l4 l5 u2 h0 h1 u3 u4 p4 u5 h2 h3 u7 u6 p5 m0 s0 "
-                "h4 d0 h5 d1 c3 d2 c4 d3 p6 d4 v0 d5 v1 d6 d7 v2 v3",
-       "back": "o0 o1 o2 f0 b0 f1 f2 b1 f3 b2 b3 o3 m0 m1 m2 h1 m3 G0 g1 g2 g3 h2 h0 h3",
-       "wait": ["w1 k0 c1 c0 s0 W1 k1 i1 k2 k3 k4 n0 y0 p0 a0 y1 p1 a1 y2 p2 a2 t0 k8 k5 L0 L1 y3 p3 t1 i0 T0 k6 k9 r0 k7 r1 b0 T1 l1 l0",
+OPT = {"aev": (), "adh": 2, "vlo": False, "sfirst": False, "plq": "S", "ca": 64, "ball": False, "afill": 1, "zfill": 1,
+       "start": "u1 c0 c1 u0 p0 e0 x0 c2 p1 e1 x1 p2 l0 l1 l2 l3 e2 x2 p3 u2 x3 e3 u3 u4 x4 p4 u5 l4 p5 h0 h1 h2 u7 u6 m0 l5 "
+                "h3 d0 d1 s0 h4 h5 c3 p6 d2 c4 d3 v0 d4 v1 d5 v2 d6 v3",
+       "back": "o0 o1 o2 f0 f1 b0 f2 b1 f3 b2 b3 o3 m0 m1 m2 h1 m3 G0 g1 g2 g3 h2 h0 h3",
+       "wait": ["w1 k0 c1 c0 s0 W1 k1 i1 k2 k3 k4 n0 y0 p0 a0 y1 p1 a1 y2 p2 t0 k8 k5 L0 L1 y3 p3 t1 i0 T0 k6 k9 r0 k7 r1 b0 T1 l1 l0",
                 "w2 c1 c0 s0 W2 i1 n0 y0 p0 y1 p1 y2 p2 t0 L0 L1 y3 p3 t1 i0 T0 r0 r1 b0 T1 l1 l0",
                 "c1 c0 s0 i1 n0 y0 p0 y1 p1 y2 p2 L0 L1 y3 p3 i0 r0 r1 b0 v0 l1 l0 d0 d1"],
-       "seq": "s0 a1 a2 d0 a3 d1 q0 d2 d3 v0 d4 d5 v1 v2 d6 v3 w0 w1 w2 w3"}
+       "seq": "s0 a1 a2 a3 d0 d2 d1 q0 v0 v1 d3 v2 v3 d4 w0 w1 w2 w3"}
 
 SCRATCH = {
     "ub": ("sbuf", [128, 512], BF), "vb": ("sbuf", [128, 512], BF), "pli": ("sbuf", [128, 72], I32),
@@ -38,7 +38,7 @@ SCRATCH = {
     "dlt": ("sbuf", [128, 40], F32), "tab": ("sbuf", [128, 384], F32),
     "ul": ("sbuf", [128, 24], U16), "prl": ("sbuf", [128, 16], U16), "gl": ("sbuf", [128, 2], U16),
     "plf": ("sbuf", [128, 72], F32), "pre": ("sbuf", [128, 256 * R], BF), "win": ("sbuf", [128, 256 * R], BF),
-    "mxv": ("sbuf", [128, 8], F32), "ltv": ("sbuf", [128, 64 * R + 64], F32), "stv": ("sbuf", [128, 64 * R + 64], F32),
+    "mxv": ("sbuf", [128, 8], F32), "ltv": ("sbuf", [128, 96 * R + 96], F32), "stv": ("sbuf", [128, 96 * R + 96], F32), "pwl": ("sbuf", [128, 2], U16),
     "of0": ("sbuf", [128, 8], U16), "g0": ("sbuf", [128, 16 * R], U16),
     "g1": ("sbuf", [128, 64 * R], BF), "g1t": ("sbuf", [128, 64 * R], BF), "fw": ("sbuf", [128, 64 * R], U16),
     "fy": ("sbuf", [128, 24 * R], U16), "iv": ("sbuf", [128, 416], BF), "inv1": ("sbuf", [128, C], BF),
@@ -200,21 +200,21 @@ def rank_program(g, core, T, topo):
     tm = lambda c: T.tmp[:, c:c + 1]
     iota(T.pi[:, 0:1], [[0, 1]], 0, 1, [("pi", 0)], small=False)
     iota(T.pi[:, 1:2], [[0, 1]], 0, 16, [("pi", 1)], small=False)
-    iota(T.pi[:, 2:3], [[0, 1]], 63, 64, [("pi", 2)], small=False)
+    iota(T.pi[:, 2:3], [[0, 1]], 1, 64, [("pi", 2)], small=False)
     iota(T.jj[:], [[1, 128]], 0, -1, ["jj"])
     iota(T.io1[:, 0:8], [[32, 4], [1, 2]], 0, 0, ["io_u"])
     iota(T.io1[:, 8:16], [[16, 8]], 2, 0, ["io_u2"])
     iota(T.io1[:, 32:40], [[-4, 2], [0, 4]], 2, 0, ["io_d0"])
     iota(T.io1[:, 40:48], [[0, 2], [-2, 2], [0, 2]], 1, 0, ["io_d1"])
     iota(T.io1[:, 16:32], [[0, 2], [1, 4], [0, 2]], 0, 0, ["io_p"])
-    iota(T.ones[:], [[0, 64]], -16, 0, ["ones"])
-    iota(T.io1[:, 48:56], [[128, 2], [16, 4]], 128, 0, ["io_s"])
+    iota(T.ones[:], [[0, 64]], 1, 0, ["ones"])
+    iota(T.io1[:, 48:56], [[16, 8]], 123, 0, ["io_s"])
     iota(T.cnt[:], [[1, C]], 0, 0, ["cnt"])
     iota(T.cn2[:], [[0, 2], [1, P2]], 0, 0, ["cn2"])
     iota(T.tab[:, 256:384], [[0, 128]], 0, 0, ["tab3", "tab4"])
-    iota(T.pw2[:], [[0, 64]], 0, 0, [("pw", s) for s in range(1, 6)])
+    iota(T.pw2[:, 0:32], [[0, 32]], 0, 0, [("pw", s) for s in range(5)])
     iota(T.bt[:], [[0, 32]], 0, 0, ["bt"])
-    for s in range(1, 6): iota(T.pw2[:, (1 << s) - 1:1 << s], [[0, 1]], -16, 0, [("pw", s)])
+    for s in range(5): iota(T.pw2[:, s:32:16], [[0, 2]], (2 << s) + 6, 0, [("pw", s)])
     iota(T.xs[:, 0:XP], [[0, XP]], 0, 0, ["pad"])
 
     ms(T.ef[:], 0.0, ["ef"])
@@ -222,8 +222,8 @@ def rank_program(g, core, T, topo):
     for col, (src, m) in enumerate(BITS):
         ts(T.ai[:, col:col + 1], T.pi[:, src:src + 1], m, None, A.bitwise_and, None, [("pi", src)], [("ai", col)])
     ms(T.dlt[:, 0:2], 0.0, [("dlt", 0)])
-    cp(T.af[:, 0:10], T.ai[:, 0:10], [("ai", c) for c in range(10)], ["af"])
     ts(T.ef[:, 3:515:4], T.jj[:], 0.0, 0.5, A.is_equal, A.mult, ["jj", "ef"], ["ef"])
+    cp(T.af[:, 0:10], T.ai[:, 0:10], [("ai", c) for c in range(10)], ["af"])
     b0, row, b16 = af(6), af(0), af(7)
 
     def qe(b): qz(*eb(b), T.ef[:, 3 - b:515 - b], ["ef"], [("e", b)])
@@ -285,26 +285,29 @@ def rank_program(g, core, T, topo):
     ]
 
     def direction(t, p0=0):
-        mx, lt, st = T.mxv[:, t:t + 1], T.ltv[:, 64 * t:64 * t + 63], T.stv[:, 64 * t:64 * t + 63]
-        last = T.stv[:, 64 * t + 62:64 * t + 63]
+        a = 96 * t + 24
+        st, last = T.stv[:, a:a + 63], T.stv[:, a + 62:a + 63]
         s = ps(0)[:, p0 + 1:p0 + 64]
         of = T.of0[:, 2 * t:2 * t + 1]
+        more = 17 if 0 < t < R else 0
+
+        def count(col, out, in_, rd):
+            op("A", lambda: act.activation(out, in_, SG, bias=last, scale=-1.0, accum_out=T.mxv[:, 2 * t + col:2 * t + col + 1]),
+               [("st", t)] + rd, [("mx", t, col)])
+
         head = [
-            lambda: op("V", lambda: vec.tensor_reduce(mx, s, AxisListType.X, A.max), [("ps", 0)], [("mx", t)]),
-            lambda: ts(lt, s, mx, 16000.0, A.is_lt, A.mult, [("ps", 0), ("mx", t)], [("lt", t)]),
-            lambda: scan(st, T.ones[:, 0:63], lt, 16000.0, A.add, A.min, ["ones", ("lt", t)], [("st", t)]),
+            lambda: scan(st, T.ones[:, 0:63], s, LOW, A.mult, A.max, ["ones", ("ps", 0)], [("st", t)]),
+            lambda: count(0, T.ltv[:, a - more:a + 63], T.stv[:, a - more:a + 63], ["six"] if more else []),
         ]
         if t > 0:
-            top = T.stw[:, 64 * t:64 * t + 63]
             return head + [
-                lambda: scan(top, T.pw2[:, 0:63], lt, 16000.0, A.add, A.min, [("pw", s) for s in range(1, 6)] + [("lt", t)], [("sw", t)]),
-                lambda: ts(of, last, tm(57), None, A.add, None, [("st", t), "chi"], [("of0", t)]),
-                lambda: ts(T.of0[:, 2 * t + 1:2 * t + 2], T.stw[:, 64 * t + 62:64 * t + 63], tm(58), None, A.add, None, [("sw", t), "clo"], [("of1", t)]),
+                lambda: count(1, T.stw[:, 16 * t:16 * t + 16], T.stv[:, a - 8:a + 62].indirect(T.pwl[:, 0:1]), ["pwl", "six"]),
+                lambda: ts(T.of0[:, 2 * t:2 * t + 2], T.mxv[:, 2 * t:2 * t + 2], 16.0, tm(57), A.mult, A.add, [("mx", t, 0), ("mx", t, 1), "w57"], [("of0", t)]),
                 lambda: cp(T.fw[:, 64 * t:64 * t + 32], T.bigt[:].indirect(T.of0[:, 2 * t:2 * t + 2]),
-                           [("bigt", 0), ("bigt", 1), ("of0", t), ("of1", t)], [("fw", t)]),
+                           [("bigt", 0), ("bigt", 1), ("of0", t)], [("fw", t)]),
             ]
         return head + [
-            lambda: ts(of, last, 1.0 / 16.0, af(9), A.mult, A.add, [("st", t), "af"], [("of0", t)]),
+            lambda: ts(of, T.mxv[:, 0:1], af(9), None, A.add, None, [("mx", t, 0), "af"], [("of0", t)]),
             lambda: cp(T.g0[:, 16 * t:16 * t + 16], T.tab[:, 0:256].indirect(of), tabs + [("of0", t)], [("g0", t)]),
             lambda: cp(T.g1[:, 64 * t:64 * t + 64], T.win[:, 256 * t:256 * t + 256].indirect(T.g0[:, 16 * t:16 * t + 4]),
                        [("win", t), ("g0", t)], [("g1", t)]),
@@ -362,10 +365,13 @@ def rank_program(g, core, T, topo):
             a = o4 + C * b
             acp(T.yp[:, a:a + C], yw(b).indirect(fyl(0)), [("yh", t, b)] + fyk(0), [("yp", t, b)])
 
-        for k in range(2):
-            for b in range(4): pair(k, b)
-            quant_piece(s0 + k)
-            send(s0 + k, lender, borrower)
+        for b in range(4): pair(0, b)
+        for b in range(OPT["zfill"]): pair(1, b)
+        quant_piece(s0)
+        send(s0, lender, borrower)
+        for b in range(OPT["zfill"], 4): pair(1, b)
+        quant_piece(s0 + 1)
+        send(s0 + 1, lender, borrower)
 
         def lend(k):
             rc, rs, keys = landed(s0 + k)
@@ -397,12 +403,14 @@ def rank_program(g, core, T, topo):
         again = direction(R)
         once = [
             lambda: (aff(tm(52), b16, 1.0 / 16.0, 0.0, ["af"], ["par"]), aff(tm(59), b0, 64.0, af(1), ["af"], ["w59"]),
-                     aff(tm(4), row, 1.0, 0.0, ["af"], ["lo4"]), ts(tm(60), row, 6.0, None, A.is_ge, None, ["af"], ["w60"])),
+                     aff(tm(4), row, 1.0, 0.0, ["af"], ["lo4"]), ts(tm(60), row, 6.0, None, A.is_ge, None, ["af"], ["w60"]),
+                     aff(tm(61), tm(60), -133.0, 256.0, ["w60"], ["w61"])),
             lambda: (ts(T.ul[:, 16:24], T.io1[:, 8:16], tm(60), -2.0, A.add, A.add, ["io_u2", "w60"], ["ul3"]),
-                     ts(T.sl[:], T.io1[:, 48:56], tm(59), tm(52), A.add, A.add, ["io_s", "w59", "par"], ["sl"]),
+                     ts(T.sl[:, 1:8], T.io1[:, 49:56], tm(59), tm(52), A.add, A.add, ["io_s", "w59", "par"], ["sl"]),
+                     ts(T.sl[:, 0:1], tm(61), tm(59), tm(52), A.add, A.add, ["w61", "w59", "par"], ["sl0"]),
                      cp(T.tab[:, 256:262], T.tmp[:, 0:6], ["lo", "lo4", "lo5"], ["tab3"]),
                      ts(T.tab[:, 320:326], T.tmp[:, 0:6], 16.0, None, A.add, None, ["lo", "lo4", "lo5"], ["tab4"])),
-            lambda: cp(T.bgl[:], T.tab[:].indirect(T.sl[:, 0:5]), tabs + ["sl", "tab3", "tab4"], ["bgl"]),
+            lambda: cp(T.bgl[:], T.tab[:].indirect(T.sl[:, 0:5]), tabs + ["sl", "sl0", "tab3", "tab4"], ["bgl"]),
             lambda: (acp(T.ups[:, 256:384], T.us[:].indirect(T.ul[:, 16:24]), ["uq", "ul3"], ["ups2"]),
                      cp(T.upc[:, 256:384].bitcast(dt.uint32), T.uc[:].bitcast(dt.uint32).indirect(T.ul[:, 16:24]), ["uq", "ul3"], ["upc2"]),
                      products(0, 128, False)),
@@ -412,7 +420,9 @@ def rank_program(g, core, T, topo):
             lambda: ts(tm(55), tm(56), tm(54), b16, A.add, A.add, ["af", "w54", "w56"], ["w55"]),
             lambda: ts(T.gl[:, 0:1], tm(55), 607.0, None, A.min, None, ["w55"], ["gl"]),
             lambda: ms(T.ad[:, 0:4 * W2:2], LOW, ["ad0"]),
-            lambda: (aff(tm(57), row, 1.0, 1008.0, ["af"], ["chi"]), aff(tm(58), row, 1.0, 1104.0, ["af"], ["clo"])),
+            lambda: (tr(T.pw2[:, 32:64], T.pw2[:, 0:32], [("pw", s) for s in range(5)], ["pwt"]), ms(T.stv[:, 96:96 * R], LOW, ["six"] + [("st", j) for j in range(1, R)]),
+                     aff(tm(57), row, 1.0, -176.0, ["af"], ["w57"]),
+                     cp(T.pwl[:, 0:1], T.pw2[:, 32:33], ["pwt"], ["pwl"])),
         ]
 
         def invert(k):
@@ -430,7 +440,7 @@ def rank_program(g, core, T, topo):
 
         def note(i):
             c = t if t else R
-            aff(T.bt[:, t:t + 1], T.stv[:, 64 * c + 62:64 * c + 63], 1.0 / 16.0, 63.0, [("st", c), "bt"], [("btc", t)])
+            aff(T.bt[:, t:t + 1], T.mxv[:, 2 * c:2 * c + 1], 1.0, -16.0 if t else 1.0, [("mx", c, 0), "bt"], [("btc", t)])
 
         def directions(i):
             if i == 0: tr(T.btt[:], T.bt[:], ["bt"] + [("btc", j) for j in range(R)], ["btt"])
@@ -499,7 +509,7 @@ def rank_program(g, core, T, topo):
                 steps = {"d": lambda i: d[i](), "s": lambda i: sign(u, (0, 1), 1, 0, C, 0), "w": lambda b: vmul(u, b, (0, 1), 2 + b, 0, C, 0)}
                 for s in OPT["seq"].split(): steps[s[0]](int(s[1]))
         else:
-            if OPT["afill"]: add(0, ca, C, (1,))
+            for b in range(OPT["afill"]): add(b, ca, C, (1,))
             pa = 128 - ca
             qz(*qx(u, 128), T.xs[:, x0 + 4 * ca - 512:x0 + 4 * ca], xkeys(u, (0,)) + (xkeys(t, (1,)) + ["pad"] if pa else []), [("qx", u)])
             nb = C if OPT["ball"] else 128

from concourse.mybir import dt, AluOpType, AxisListType, ActivationFunctionType

C, P2, R = 192, 96, 3
X4, U8, U16, BF, F32, I32 = "float8_e4m3fn_x4", "uint8", "uint16", "bfloat16", "float32", "int32"
NSEG = 4 * R
W2 = 2 * C
XP = 256
BIG, HALF = 16 * (64 + 6), 576
LOW = -1.0e29
TINY = 2.0 ** -120
OPT = {"aev": (), "adh": 2, "vlo": False, "sfirst": False, "plq": "S", "ca": 64, "ball": False, "afill": 1, "zfill": 1,
       "start": "u1 c0 c1 u0 p0 e0 x0 c2 p1 e1 x1 p2 l0 l1 l2 l3 e2 x2 p3 u2 x3 e3 u3 u4 x4 p4 u5 l4 p5 h0 h1 h2 u7 u6 m0 l5 "
                "h3 d0 d1 s0 h4 h5 c3 p6 d2 c4 d3 v0 d4 v1 d5 v2 d6 v3",
       "back": "o0 o1 o2 f0 f1 b0 f2 b1 f3 b2 b3 o3 m0 m1 m2 h1 m3 G0 g1 g2 g3 h2 h0 h3",
       "wait": ["w1 k0 c1 c0 s0 W1 k1 i1 k2 k3 k4 n0 y0 p0 a0 y1 p1 a1 y2 p2 t0 k8 k5 L0 L1 y3 p3 t1 i0 T0 k6 k9 r0 k7 r1 b0 T1 l1 l0",
                "w2 c1 c0 s0 W2 i1 n0 y0 p0 y1 p1 y2 p2 t0 L0 L1 y3 p3 t1 i0 T0 r0 r1 b0 T1 l1 l0",
                "c1 c0 s0 i1 n0 y0 p0 y1 p1 y2 p2 L0 L1 y3 p3 i0 r0 r1 b0 v0 l1 l0 d0 d1"],
       "seq": "s0 a1 a2 a3 d0 d2 d1 q0 v0 v1 d3 v2 v3 d4 w0 w1 w2 w3"}

SCRATCH = {
    "ub": ("sbuf", [128, 512], BF), "vb": ("sbuf", [128, 512], BF), "pli": ("sbuf", [128, 72], I32),
    "w0c": ("sbuf", [128, 512], X4), "w0s": ("sbuf", [128, 512], U8),
    "w1c": ("sbuf", [128, 512], X4), "w1s": ("sbuf", [128, 512], U8),
    "uc": ("sbuf", [128, 128], X4), "us": ("sbuf", [128, 128], U8),
    "upc": ("sbuf", [128, 384], X4), "ups": ("sbuf", [128, 384], U8),
    "vc": ("sbuf", [128, 128], X4), "vs": ("sbuf", [128, 128], U8),
    "tl": ("sbuf", [128, 4 * C + 4 * P2 * NSEG], BF), "xs": ("sbuf", [128, XP + 4 * C * R], BF),
    "lc": ("sbuf", [128, C + P2 * NSEG], X4), "ls": ("sbuf", [128, C + P2 * NSEG], U8),
    "sc": ("sbuf", [128, 128 * NSEG], X4), "ss": ("sbuf", [128, 128 * NSEG], U8),
    "qc": ("sbuf", [128, C * R], X4), "qs": ("sbuf", [128, C * R], U8),
    "dc": ("sbuf", [128, C * R], X4), "ds": ("sbuf", [128, C * R], U8),
    "jj": ("sbuf", [128, 128], BF), "ef": ("sbuf", [128, 520], BF),
    "ec": ("sbuf", [128, 512], X4), "es": ("sbuf", [128, 512], U8),
    "pi": ("sbuf", [128, 8], I32), "ai": ("sbuf", [128, 16], I32), "af": ("sbuf", [128, 16], F32),
    "tmp": ("sbuf", [128, 96], F32), "ones": ("sbuf", [128, 64], F32),
    "sl": ("sbuf", [128, 8], U16), "bgl": ("sbuf", [128, 80], U16), "pw2": ("sbuf", [128, 64], F32), "stw": ("sbuf", [128, 64 * R + 64], F32), "big": ("sbuf", [128, BIG], BF), "bigt": ("sbuf", [128, BIG], BF),
    "io1": ("sbuf", [128, 56], F32), "cnt": ("sbuf", [128, C], BF),
    "dlt": ("sbuf", [128, 40], F32), "tab": ("sbuf", [128, 384], F32),
    "ul": ("sbuf", [128, 24], U16), "prl": ("sbuf", [128, 16], U16), "gl": ("sbuf", [128, 2], U16),
    "plf": ("sbuf", [128, 72], F32), "pre": ("sbuf", [128, 256 * R], BF), "win": ("sbuf", [128, 256 * R], BF),
    "mxv": ("sbuf", [128, 8], F32), "ltv": ("sbuf", [128, 96 * R + 96], F32), "stv": ("sbuf", [128, 96 * R + 96], F32), "pwl": ("sbuf", [128, 2], U16),
    "of0": ("sbuf", [128, 8], U16), "g0": ("sbuf", [128, 16 * R], U16),
    "g1": ("sbuf", [128, 64 * R], BF), "g1t": ("sbuf", [128, 64 * R], BF), "fw": ("sbuf", [128, 64 * R], U16),
    "fy": ("sbuf", [128, 24 * R], U16), "iv": ("sbuf", [128, 416], BF), "inv1": ("sbuf", [128, C], BF),
    "cn2": ("sbuf", [128, C], BF), "ivt": ("sbuf", [128, 800], BF), "bl": ("sbuf", [128, 32 * R], U16),
    "bt": ("sbuf", [128, 32], F32), "btt": ("sbuf", [128, 32], F32), "odt": ("sbuf", [128, 4], F32),
    "sg": ("sbuf", [128, C * R], BF), "sh": ("sbuf", [128, C * R], BF),
    "vv": ("sbuf", [128, 4 * C * R], BF), "lo": ("sbuf", [128, 4 * C * R], BF),
    "yh": ("sbuf", [128, 4 * C * R], BF), "yp": ("sbuf", [128, 4 * C * R], BF), "dh": ("sbuf", [128, 4 * P2 * R], BF),
    "pq": ("sbuf", [128, 4 * W2 * R], BF), "ad": ("sbuf", [128, 4 * W2], BF), "mo": ("sbuf", [128, 4 * W2 * R], BF),
    "mc2": ("sbuf", [128, 4 * C], BF), "yo": ("sbuf", [128, C], F32),
}
for _b in range(8):
    SCRATCH["ps%d" % _b] = ("psum", [128, 512], F32)

LOADS = ["pl", "u", "x", "wc", "ws", "mc", "ms", "v"]
SEMAPHORES = (["eV", "eA", "eP", "eG", "sent", "st"] + ["ld_" + n for n in LOADS] + ["arr%d" % s for s in range(NSEG)])


def emit(ops, queues, T, finals, landing):
    writer, readers = {}, {}
    clock = {q: {} for q in queues}
    count = {q: 0 for q in queues}
    done = {}
    needed = set()
    plan = []
    for eng, fn, rd, wr, tok in ops:
        deps = []
        for k in rd:
            if k in writer: deps.append(writer[k])
            if k[0] == "arr": deps.append(("arr%d" % k[1], landing[k[1]]))
            if k[0] == "ps": deps += [t for t in readers.get(k, []) if t[0] != eng]
        for k in wr:
            if k in writer: deps.append(writer[k])
            deps += readers.get(k, [])
        want = {}
        for s, i in deps:
            want[s] = max(want.get(s, 0), i)
        waits = []
        for s in sorted(want, key=lambda s: -len(done.get((s, want[s]), {}))):
            if clock[eng].get(s, 0) >= want[s]: continue
            waits.append((s, want[s]))
            needed.add((s, want[s]))
            clock[eng][s] = want[s]
            for a, b in done.get((s, want[s]), {}).items():
                clock[eng][a] = max(clock[eng].get(a, 0), b)
        if tok is None:
            count[eng] += 1
            me = (eng, count[eng])
        else:
            me = tok
        done[me] = dict(clock[eng])
        for k in rd: readers.setdefault(k, []).append(me)
        for k in wr:
            writer[k] = me
            readers[k] = []
        plan.append((eng, fn, waits, me, tok))
    value, total = {}, {q: 0 for q in queues}
    for eng, fn, waits, me, tok in plan:
        if tok is None and me in needed:
            total[eng] += 1
            value[me] = total[eng]
    for eng, fn, waits, me, tok in plan:
        for s, i in waits:
            if s in queues: queues[eng].wait_ge(T.sem["e" + s], value[(s, i)])
            else: queues[eng].wait_ge(T.sem[s], i)
        ins = fn()
        if tok is None:
            if me in needed: ins.then_inc(T.sem["e" + eng], 1)
        elif tok[0] != "remote":
            ins.then_inc(T.sem[tok[0]], 16)
    for s, v in finals:
        queues["G"].wait_ge(T.sem[s], v)


def rank_program(g, core, T, topo):
    rank = T.rank_of(core)
    if rank is None:
        return
    n_ranks = len(T.cores)
    A = AluOpType
    ID, CP, SG = ActivationFunctionType.Identity, ActivationFunctionType.Copy, ActivationFunctionType.Sign
    vec, act, pe, syn = g.vector, g.scalar, g.tensor, g.sync
    queues = {"V": vec, "A": act, "P": pe, "G": g, "S": syn}
    ops = []
    stores, sent, landing = [0], [0], {}

    def op(eng, fn, rd, wr, tok=None):
        ops.append((eng, fn, [k if isinstance(k, tuple) else (k,) for k in rd], [k if isinstance(k, tuple) else (k,) for k in wr], tok))

    def ts(out, in0, s1, s2, o0, o1, rd, wr):
        if s2 is None: op("V", lambda: vec.tensor_scalar(out, in0, s1, None, o0), rd, wr)
        else: op("V", lambda: vec.tensor_scalar(out, in0, s1, s2, o0, o1), rd, wr)

    def tt(out, in0, in1, o, rd, wr): op("V", lambda: vec.tensor_tensor(out, in0, in1, o), rd, wr)
    def cp(out, in_, rd, wr): op("V", lambda: vec.tensor_copy(out, in_), rd, wr)
    def ms(out, c, wr): op("V", lambda: vec.memset(out, c), [], wr)
    def tr(out, in_, rd, wr): op("V", lambda: vec.transpose(out, in_), rd, wr)
    def qz(oc, os_, in_, rd, wr): op("V", lambda: vec.quantize_mx(oc, os_, in_), rd, wr)
    def scan(out, d0, d1, init, o0, o1, rd, wr): op("V", lambda: vec.tensor_tensor_scan(out, d0, d1, init, o0, o1), rd, wr)
    def acp(out, in_, rd, wr): op("A", lambda: act.activation(out, in_, CP), rd, wr)
    def asc(out, in_, s, rd, wr): op("A", lambda: act.activation(out, in_, CP, scale=s), rd, wr)
    def aff(out, in_, s, b, rd, wr): op("A", lambda: act.activation(out, in_, ID, bias=b, scale=s), rd, wr)
    def mm(out, lc_, ls_, rc, rs, rd, wr): op("P", lambda: pe.matmul_mx(out, lc_, ls_, rc, rs, True, True), rd, wr)
    def iota(out, pat, base, cm, wr, small=True):
        if small: op("G", lambda: g.iota(out, pat, base, cm, allow_small_or_imprecise_dtypes=True), [], wr)
        else: op("G", lambda: g.iota(out, pat, base, cm), [], wr)
    def load(eng, out, name, rd=()): op(eng, lambda: queues[eng].dma_start(out, T[name][:]), list(rd), ["in_" + name], ("ld_" + name, 16))
    def store(eng, out, in_, rd):
        stores[0] += 16
        op(eng, lambda: queues[eng].dma_start(out, in_), rd, [], ("st", stores[0]))
    def ps(b): return T["ps%d" % b]

    def send(seg, to, frm):
        rid, pid, _ = topo.addr(to)
        mask = topo.mask(core, to)
        a, l = 128 * seg + 32, C + P2 * seg
        sent[0] += 2 * len(topo.engines(core, to))
        landing[seg] = 2 * len(topo.engines(frm, core))
        sides = [(T.lc[:, l:l + P2].bitcast(dt.uint8), T.sc[:, a:a + P2].bitcast(dt.uint8)), (T.ls[:, l:l + P2], T.ss[:, a:a + P2])]
        if OPT["sfirst"]: sides.reverse()
        for i, (dst, src) in enumerate(sides):
            op("G", lambda dst=dst, src=src: g.remote_dma(dst, src, T.sem["arr%d" % seg], T.sem.sent, pid, rid, mask),
               [("sc", seg)], [], ("remote", 2 * seg + 1 + i))

    def tile_at(seg): return 4 * C + 4 * P2 * seg
    def tile_keys(seg): return [("tl", seg, b) for b in range(4)] if seg >= 0 else ["in_x"]

    def quant_piece(seg):
        e = tile_at(seg + 1)
        qz(T.sc[:, 128 * seg:128 * seg + 128], T.ss[:, 128 * seg:128 * seg + 128], T.tl[:, e - 512:e],
           tile_keys(seg) + tile_keys(seg - 1), [("sc", seg)])

    def landed(seg):
        e = C + P2 * (seg + 1)
        return T.lc[:, e - 128:e], T.ls[:, e - 128:e], [("arr", seg), ("arr", seg - 1) if seg > 0 else ("qx", 0)]

    def got(bank): return ps(bank)[:, 32:128]

    def qx(t, n=C):
        return (T.lc[:, 0:n], T.ls[:, 0:n]) if t == 0 else (T.qc[:, C * (t - 1):C * (t - 1) + n], T.qs[:, C * (t - 1):C * (t - 1) + n])

    def xcol(t, b, c0=0, c1=C):
        o = XP + 4 * C * (t - 1)
        return T.tl[:, b:4 * C:4] if t == 0 else T.xs[:, o + 4 * c0 + b:o + 4 * c1:4]

    def xkeys(t, parts=(0, 1)): return ["in_x"] if t == 0 else [("xs", t, b, c) for b in range(4) for c in parts]
    def eb(b): return T.ec[:, 128 * b:128 * b + 128], T.es[:, 128 * b:128 * b + 128]

    load("A", T.ub[:], "u")
    if OPT["plq"] == "S": load("S", T.pli[:], "pl")
    load("S", T.tl[:, 0:4 * C], "x")
    if OPT["plq"] == "A": load("A", T.pli[:], "pl")
    load("S", T.w0c[:].bitcast(dt.uint8), "wc")
    load("S", T.w0s[:], "ws")
    load("S", T.w1c[:].bitcast(dt.uint8), "mc")
    load("S", T.w1s[:], "ms")

    af = lambda c: T.af[:, c:c + 1]
    tm = lambda c: T.tmp[:, c:c + 1]
    iota(T.pi[:, 0:1], [[0, 1]], 0, 1, [("pi", 0)], small=False)
    iota(T.pi[:, 1:2], [[0, 1]], 0, 16, [("pi", 1)], small=False)
    iota(T.pi[:, 2:3], [[0, 1]], 1, 64, [("pi", 2)], small=False)
    iota(T.jj[:], [[1, 128]], 0, -1, ["jj"])
    iota(T.io1[:, 0:8], [[32, 4], [1, 2]], 0, 0, ["io_u"])
    iota(T.io1[:, 8:16], [[16, 8]], 2, 0, ["io_u2"])
    iota(T.io1[:, 32:40], [[-4, 2], [0, 4]], 2, 0, ["io_d0"])
    iota(T.io1[:, 40:48], [[0, 2], [-2, 2], [0, 2]], 1, 0, ["io_d1"])
    iota(T.io1[:, 16:32], [[0, 2], [1, 4], [0, 2]], 0, 0, ["io_p"])
    iota(T.ones[:], [[0, 64]], 1, 0, ["ones"])
    iota(T.io1[:, 48:56], [[16, 8]], 123, 0, ["io_s"])
    iota(T.cnt[:], [[1, C]], 0, 0, ["cnt"])
    iota(T.cn2[:], [[0, 2], [1, P2]], 0, 0, ["cn2"])
    iota(T.tab[:, 256:384], [[0, 128]], 0, 0, ["tab3", "tab4"])
    iota(T.pw2[:, 0:32], [[0, 32]], 0, 0, [("pw", s) for s in range(5)])
    iota(T.bt[:], [[0, 32]], 0, 0, ["bt"])
    for s in range(5): iota(T.pw2[:, s:32:16], [[0, 2]], (2 << s) + 6, 0, [("pw", s)])
    iota(T.xs[:, 0:XP], [[0, XP]], 0, 0, ["pad"])

    ms(T.ef[:], 0.0, ["ef"])
    BITS = [(0, 15), (0, 14), (0, 12), (0, 8), (0, 4), (0, 2), (0, 1), (0, 16), (1, 16), (2, 255)]
    for col, (src, m) in enumerate(BITS):
        ts(T.ai[:, col:col + 1], T.pi[:, src:src + 1], m, None, A.bitwise_and, None, [("pi", src)], [("ai", col)])
    ms(T.dlt[:, 0:2], 0.0, [("dlt", 0)])
    ts(T.ef[:, 3:515:4], T.jj[:], 0.0, 0.5, A.is_equal, A.mult, ["jj", "ef"], ["ef"])
    cp(T.af[:, 0:10], T.ai[:, 0:10], [("ai", c) for c in range(10)], ["af"])
    b0, row, b16 = af(6), af(0), af(7)

    def qe(b): qz(*eb(b), T.ef[:, 3 - b:515 - b], ["ef"], [("e", b)])

    WT = [1, 2, 4, 8, 32, 64]
    dl = lambda a, b: T.dlt[:, 1 + a:1 + b]

    def double(s):
        w = 1 << s
        rd = [("dlt", i) for i in range(s + 1)]
        if s < 4: ts(dl(w, 2 * w), dl(0, w), float(WT[s]), tm(43 - s), A.add, A.subtract, rd + ["a2"], [("dlt", s + 1)])
        else: ts(dl(w, 2 * w), dl(0, w), float(WT[s]), None, A.add, None, rd, [("dlt", s + 1)])

    lowat = lambda h: row if h == 4 else tm(h)

    def low(h):
        a, w = (0, 2) if h == 0 else (1 << h, 2 << h)
        aff(T.tab[:, a:w], T.jj[:, a:w], 0.0, lowat(h), ["jj", "af", "lo", "lo5"], [("tab", 0, h)])

    def high(h):
        w = 1 << h
        a = 0 if h else 1
        ts(T.tab[:, 128 + w - a:128 + 2 * w], dl(-a, w), lowat(h), float(WT[h]), A.add, A.add,
           [("dlt", i) for i in range(h + 1)] + ["af", "lo", "lo5"], [("tab", 1, h)])

    tabs = [("tab", i, h) for i in range(2) for h in range(6)] + ["tab1", "tab2"]
    consts = [
        lambda: ts(T.tmp[:, 40:44], T.af[:, 3:7], 2.0, None, A.mult, None, ["af"], ["a2"]),
        lambda: aff(tm(5), row, 1.0, 128.0, ["af"], ["lo5"]),
        lambda: ts(T.tmp[:, 0:4], T.af[:, 0:4], row, tm(40), A.add, A.add, ["af", "a2"], ["lo"]),
        lambda: ts(T.tab[:, 64:128], T.tab[:, 0:64], 16.0, None, A.add, None, tabs[0:6], ["tab1"]),
        lambda: ts(T.tab[:, 192:256], T.tab[:, 128:192], 16.0, None, A.add, None, tabs[6:12], ["tab2"]),
    ]
    places = [
        lambda: ts(tm(34), row, b0, 10.0, A.subtract, A.min, ["af"], ["t34"]),
        lambda: ts(T.tmp[:, 48:64], T.io1[:, 32:48], b0, tm(34), A.mult, A.add, ["io_d0", "io_d1", "af", "t34"], ["p1"]),
        lambda: tt(T.tmp[:, 64:80], T.tmp[:, 48:64], T.io1[:, 16:32], A.add, ["p1", "io_p"], ["p2"]),
        lambda: ts(T.prl[:], T.tmp[:, 64:80], tm(34), None, A.add, None, ["p2", "t34"], ["prl"]),
        lambda: cp(T.plf[:], T.pli[:], ["in_pl"], ["plf"]),
        lambda: windows(0),
        lambda: windows2(0),
    ]

    def windows(t):
        acp(T.pre[:, 256 * t:256 * t + 256], T.plf[:, 24 * t:24 * t + 24].indirect(T.prl[:]), ["plf", "prl"], [("pre", t)])

    def windows2(t):
        tr(T.win[:, 256 * t:256 * t + 256], T.pre[:, 256 * t:256 * t + 256], [("pre", t)], [("win", t)])

    picks = [
        lambda: ts(T.ul[:, 0:8], T.io1[:, 0:8], af(8), None, A.add, None, ["io_u", "af"], ["ul"]),
        lambda: cp(T.ul[:, 8:16], T.io1[:, 8:16], ["io_u2"], ["ul2"]),
        lambda: qz(T.uc[:], T.us[:], T.ub[:], ["in_u"], ["uq"]),
        lambda: acp(T.ups[:, 0:128], T.us[:].indirect(T.ul[:, 0:8]), ["uq", "ul"], ["ups0"]),
        lambda: cp(T.upc[:, 0:128].bitcast(dt.uint32), T.uc[:].bitcast(dt.uint32).indirect(T.ul[:, 0:8]), ["uq", "ul"], ["upc0"]),
        lambda: acp(T.ups[:, 128:256], T.us[:].indirect(T.ul[:, 8:16]), ["uq", "ul2"], ["ups1"]),
        lambda: cp(T.upc[:, 128:256].bitcast(dt.uint32), T.uc[:].bitcast(dt.uint32).indirect(T.ul[:, 8:16]), ["uq", "ul2"], ["upc1"]),
        lambda: qz(*qx(0), T.tl[:, 0:4 * C], ["in_x"], [("qx", 0)]),
    ]

    def direction(t, p0=0):
        a = 96 * t + 24
        st, last = T.stv[:, a:a + 63], T.stv[:, a + 62:a + 63]
        s = ps(0)[:, p0 + 1:p0 + 64]
        of = T.of0[:, 2 * t:2 * t + 1]
        more = 17 if 0 < t < R else 0

        def count(col, out, in_, rd):
            op("A", lambda: act.activation(out, in_, SG, bias=last, scale=-1.0, accum_out=T.mxv[:, 2 * t + col:2 * t + col + 1]),
               [("st", t)] + rd, [("mx", t, col)])

        head = [
            lambda: scan(st, T.ones[:, 0:63], s, LOW, A.mult, A.max, ["ones", ("ps", 0)], [("st", t)]),
            lambda: count(0, T.ltv[:, a - more:a + 63], T.stv[:, a - more:a + 63], ["six"] if more else []),
        ]
        if t > 0:
            return head + [
                lambda: count(1, T.stw[:, 16 * t:16 * t + 16], T.stv[:, a - 8:a + 62].indirect(T.pwl[:, 0:1]), ["pwl", "six"]),
                lambda: ts(T.of0[:, 2 * t:2 * t + 2], T.mxv[:, 2 * t:2 * t + 2], 16.0, tm(57), A.mult, A.add, [("mx", t, 0), ("mx", t, 1), "w57"], [("of0", t)]),
                lambda: cp(T.fw[:, 64 * t:64 * t + 32], T.bigt[:].indirect(T.of0[:, 2 * t:2 * t + 2]),
                           [("bigt", 0), ("bigt", 1), ("of0", t)], [("fw", t)]),
            ]
        return head + [
            lambda: ts(of, T.mxv[:, 0:1], af(9), None, A.add, None, [("mx", t, 0), "af"], [("of0", t)]),
            lambda: cp(T.g0[:, 16 * t:16 * t + 16], T.tab[:, 0:256].indirect(of), tabs + [("of0", t)], [("g0", t)]),
            lambda: cp(T.g1[:, 64 * t:64 * t + 64], T.win[:, 256 * t:256 * t + 256].indirect(T.g0[:, 16 * t:16 * t + 4]),
                       [("win", t), ("g0", t)], [("g1", t)]),
            lambda: tr(T.g1t[:, 64 * t:64 * t + 64], T.g1[:, 64 * t:64 * t + 64], [("g1", t)], [("g1t", t)]),
            lambda: cp(T.fw[:, 64 * t:64 * t + 64], T.g1t[:, 64 * t:64 * t + 64], [("g1t", t)], [("fw", t)]),
        ]

    def sign(t, part, bank, c0, c1, p0):
        op("A", lambda: act.activation(T.sg[:, C * t + c0:C * t + c1], ps(bank)[:, p0:p0 + c1 - c0], SG, bias=-TINY), [("ps", bank)], [("sg", t, c) for c in part])

    def vmul(t, b, part, bank, c0, c1, p0):
        a = 4 * C * t + C * b
        tt(T.vv[:, a + c0:a + c1], ps(bank)[:, p0:p0 + c1 - c0], T.sg[:, C * t + c0:C * t + c1], A.mult,
           [("ps", bank)] + [("sg", t, c) for c in part], [("vv", t, b, c) for c in part])

    def products(t, n, everything=True):
        xa, xn, kq = qx(t, 128), qx(t, n), [("qx", t)]
        if t == 0 and everything: mm(ps(0)[:, 0:128], T.upc[:, 0:128], T.ups[:, 0:128], *xa, kq + ["upc0", "ups0"], [("ps", 0)])
        else: mm(ps(0)[:, 0:128], T.upc[:, 256:384], T.ups[:, 256:384], *xa, kq + ["upc2", "ups2"], [("ps", 0)])
        if not everything: return
        mm(ps(1)[:, 0:n], T.upc[:, 128:256], T.ups[:, 128:256], *xn, kq + ["upc1", "ups1"], [("ps", 1)])
        for b in range(4):
            mm(ps(2 + b)[:, 0:n], *eb(b), *xn, kq + [("e", b)], [("ps", 2 + b)])

    d = direction(0)
    steps = {"c": lambda i: consts[i](), "p": lambda i: places[i](), "u": lambda i: picks[i](), "e": qe, "x": double, "l": low, "h": high,
             "m": lambda i: products(0, C), "s": lambda i: sign(0, (0, 1), 1, 0, C, 0), "d": lambda i: d[i](),
             "v": lambda b: vmul(0, b, (0, 1), 2 + b, 0, C, 0)}
    for s in OPT["start"].split(): steps[s[0]](int(s[1]))

    for t in range(R):
        lender = T.cores[(rank + 1 + t) % n_ranks]
        borrower = T.cores[(rank - 1 - t) % n_ranks]
        o4, o8, s0 = 4 * C * t, 4 * W2 * t, 4 * t
        fwa = lambda k, side, t=t: 64 * t + (32 * side + 22 * k if t == 0 else 16 * (1 - side) + 6 * k)
        fwl = lambda k, side: T.fw[:, fwa(k, side):fwa(k, side) + 6]
        fyl = lambda k, t=t: T.fy[:, 24 * t + 12 * k:24 * t + 12 * k + 12]
        fyk = lambda k, t=t: [("fy", t, k, 0), ("fy", t, k, 1)]

        def pair(k, b):
            z0 = tile_at(s0 + k)
            w = T.vv[:, o4 + C * b:o4 + C * b + C]
            l = T.lo[:, o4 + 4 * P2 * k + P2 * b:o4 + 4 * P2 * k + P2 * b + P2]
            vk = [("vv", t, b, 0), ("vv", t, b, 1), ("fw", t)]
            (cp if OPT["vlo"] and k == 0 and b == 0 else acp)(l, w.indirect(fwl(k, 0)), vk, [("lo", t, k, b)])
            tt(T.tl[:, z0 + b:z0 + 4 * P2:4], w.indirect(fwl(k, 1)), l, A.add, vk + [("lo", t, k, b)], [("tl", s0 + k, b)])

        yw = lambda b, c0=0, c1=C: T.yh[:, o4 + C * b + c0:o4 + C * b + c1]
        sgh = T.sh[:, C * t:C * t + C]

        def ymul(b):
            tt(yw(b), xcol(t, b), sgh, A.mult, xkeys(t) + [("sh", t)], [("yh", t, b)])

        def yperm(b):
            a = o4 + C * b
            acp(T.yp[:, a:a + C], yw(b).indirect(fyl(0)), [("yh", t, b)] + fyk(0), [("yp", t, b)])

        for b in range(4): pair(0, b)
        for b in range(OPT["zfill"]): pair(1, b)
        quant_piece(s0)
        send(s0, lender, borrower)
        for b in range(OPT["zfill"], 4): pair(1, b)
        quant_piece(s0 + 1)
        send(s0 + 1, lender, borrower)

        def lend(k):
            rc, rs, keys = landed(s0 + k)
            wc_, ws_, wk = (T.w0c, T.w0s, ["in_wc", "in_ws"]) if k == 0 else (T.w1c, T.w1s, ["in_mc", "in_ms"])
            h0 = tile_at(s0 + 2 + k)
            for b in range(4):
                mm(ps(4 * k + b)[:, 0:128], wc_[:, 128 * b:128 * b + 128], ws_[:, 128 * b:128 * b + 128], rc, rs, keys + wk, [("ps", 4 * k + b)])
            for b in range(4):
                o, i = T.tl[:, h0 + b:h0 + 4 * P2:4], got(4 * k + b)
                if b in OPT["aev"]: asc(o, i, 0.03125, [("ps", 4 * k + b)], [("tl", s0 + 2 + k, b)])
                else: ts(o, i, 0.03125, None, A.mult, None, [("ps", 4 * k + b)], [("tl", s0 + 2 + k, b)])
            quant_piece(s0 + 2 + k)
            send(s0 + 2 + k, borrower, lender)

        def table(i):
            if t + 1 == R: return
            a, e = (0, HALF) if i == 0 else (HALF, BIG)
            acp(T.big[:, a:e], T.win[:, 256 * (t + 1):256 * (t + 2)].indirect(T.bgl[:, a // 16:e // 16]), [("win", t + 1), "bgl"], [("big", i)])

        def table2(i):
            if t + 1 == R: return
            a, e = (0, HALF) if i == 0 else (HALF, BIG)
            tr(T.bigt[:, a:e], T.big[:, a:e], [("big", i)], [("bigt", i)])

        def compact(k):
            for e in range(2):
                cp(T.fy[:, 24 * t + 12 * k + 6 * e:24 * t + 12 * k + 6 * e + 6], fwl(k, e), [("fw", t)], [("fy", t, k, e)])

        again = direction(R)
        once = [
            lambda: (aff(tm(52), b16, 1.0 / 16.0, 0.0, ["af"], ["par"]), aff(tm(59), b0, 64.0, af(1), ["af"], ["w59"]),
                     aff(tm(4), row, 1.0, 0.0, ["af"], ["lo4"]), ts(tm(60), row, 6.0, None, A.is_ge, None, ["af"], ["w60"]),
                     aff(tm(61), tm(60), -133.0, 256.0, ["w60"], ["w61"])),
            lambda: (ts(T.ul[:, 16:24], T.io1[:, 8:16], tm(60), -2.0, A.add, A.add, ["io_u2", "w60"], ["ul3"]),
                     ts(T.sl[:, 1:8], T.io1[:, 49:56], tm(59), tm(52), A.add, A.add, ["io_s", "w59", "par"], ["sl"]),
                     ts(T.sl[:, 0:1], tm(61), tm(59), tm(52), A.add, A.add, ["w61", "w59", "par"], ["sl0"]),
                     cp(T.tab[:, 256:262], T.tmp[:, 0:6], ["lo", "lo4", "lo5"], ["tab3"]),
                     ts(T.tab[:, 320:326], T.tmp[:, 0:6], 16.0, None, A.add, None, ["lo", "lo4", "lo5"], ["tab4"])),
            lambda: cp(T.bgl[:], T.tab[:].indirect(T.sl[:, 0:5]), tabs + ["sl", "sl0", "tab3", "tab4"], ["bgl"]),
            lambda: (acp(T.ups[:, 256:384], T.us[:].indirect(T.ul[:, 16:24]), ["uq", "ul3"], ["ups2"]),
                     cp(T.upc[:, 256:384].bitcast(dt.uint32), T.uc[:].bitcast(dt.uint32).indirect(T.ul[:, 16:24]), ["uq", "ul3"], ["upc2"]),
                     products(0, 128, False)),
            lambda: (ms(T.iv[:], 0.0, ["inv0", "nw"]), ts(tm(53), b0, 32.0, 384.0, A.mult, A.add, ["af"], ["w53"])),
            lambda: (ts(tm(54), row, b0, 16.0, A.subtract, A.mult, ["af"], ["w54"]),
                     ts(tm(56), b0, tm(52), tm(53), A.not_equal, A.mult, ["af", "par", "w53"], ["w56"])),
            lambda: ts(tm(55), tm(56), tm(54), b16, A.add, A.add, ["af", "w54", "w56"], ["w55"]),
            lambda: ts(T.gl[:, 0:1], tm(55), 607.0, None, A.min, None, ["w55"], ["gl"]),
            lambda: ms(T.ad[:, 0:4 * W2:2], LOW, ["ad0"]),
            lambda: (tr(T.pw2[:, 32:64], T.pw2[:, 0:32], [("pw", s) for s in range(5)], ["pwt"]), ms(T.stv[:, 96:96 * R], LOW, ["six"] + [("st", j) for j in range(1, R)]),
                     aff(tm(57), row, 1.0, -176.0, ["af"], ["w57"]),
                     cp(T.pwl[:, 0:1], T.pw2[:, 32:33], ["pwt"], ["pwl"])),
        ]

        def invert(k):
            if k: cp(T.inv1[:].indirect(fyl(1)), T.cn2[:], ["cn2"] + fyk(1), ["inv1"])
            else: cp(T.iv[:, 16:16 + C].indirect(fyl(0)), T.cnt[:], ["cnt"] + fyk(0), ["inv0"])

        def turn(i):
            if i: tr(T.ivt[:, 384:800], T.iv[:], ["inv0", "nw"], ["ivB"])
            else: tr(T.ivt[:, 0:384], T.iv[:, 16:400], ["inv0", "nw"], ["ivA"])

        def lists(k):
            a = 32 * t + 16 * (1 - k)
            if k: cp(T.bl[:, a:a + 16], T.ivt[:, C:800].indirect(T.gl[:, 0:1]), ["ivA", "ivB", "gl"], [("bl", t, 1)])
            else: ts(T.bl[:, a:a + 16], T.ivt[:].indirect(T.gl[:, 0:1]), 2.0, 1.0, A.mult, A.add, ["ivA", "ivB", "gl"], [("bl", t, 0)])

        def note(i):
            c = t if t else R
            aff(T.bt[:, t:t + 1], T.mxv[:, 2 * c:2 * c + 1], 1.0, -16.0 if t else 1.0, [("mx", c, 0), "bt"], [("btc", t)])

        def directions(i):
            if i == 0: tr(T.btt[:], T.bt[:], ["bt"] + [("btc", j) for j in range(R)], ["btt"])
            if i == 1:
                for k in range(2):
                    cp(T.odt[:, k:4:2], T.btt[:, 6 * k:32:16], ["btt"], [("odt", k)])
                for gr in range(8):
                    store("S", T.od[gr:gr + 1, :], T.odt[32 * (gr // 2):32 * (gr // 2) + R, 2 * (gr % 2):2 * (gr % 2) + 2], [("odt", 0), ("odt", 1)])

        if t == 0: load("S", T.vb[:], "v", [("sc", 1)])
        steps = {"c": compact, "i": invert, "y": ymul, "p": yperm, "t": table, "T": table2, "r": turn, "l": lists, "b": note, "L": lend,
                 "s": lambda i: ts(sgh, T.sg[:, C * t:C * t + C], 0.5, None, A.mult, None, [("sg", t, 0), ("sg", t, 1)], [("sh", t)]),
                 "n": lambda i: acp(T.iv[:, 208:208 + C], T.inv1[:].indirect(fyl(0)), ["inv1"] + fyk(0), ["nw"]),
                 "w": windows, "W": windows2, "k": lambda i: once[i](), "a": lambda i: again[i](), "d": directions,
                 "v": lambda i: qz(T.vc[:], T.vs[:], T.vb[:], ["in_v"], ["vq"])}
        for s in OPT["wait"][t].split(): steps[s[0]](int(s[1]))
        l1 = T.bl[:, 32 * t:32 * t + 12]
        for k in range(2):
            rc, rs, keys = landed(s0 + 2 + k)
            for b in range(4):
                mm(ps(4 * k + b)[:, 0:128], *eb(b), rc, rs, keys + [("e", b)], [("ps", 4 * k + b)])
        dh = lambda b: T.dh[:, 4 * P2 * t + P2 * b:4 * P2 * t + P2 * (b + 1)]

        def bring(b):
            acp(T.ad[:, W2 * b + 1:W2 * (b + 1):2], dh(b).indirect(l1), [("dh", t, b), ("bl", t, 1), "ad0"], [("ad", b)])

        def order(b):
            for e in range(2):
                a, y = o8 + W2 * b + C * e, T.yp[:, o4 + C * b + P2 * e:o4 + C * b + P2 * (e + 1)]
                tt(T.pq[:, a:a + C:2], got(b), y, A.max, [("ps", b), ("yp", t, b)], [("pq", t, b, e, 0)])
                tt(T.pq[:, a + 1:a + C:2], got(b), y, A.min, [("ps", b), ("yp", t, b)], [("pq", t, b, e, 1)])

        def fetch(b): (acp if b < OPT["adh"] else cp)(dh(b), got(4 + b), [("ps", 4 + b)], [("dh", t, b)])

        def middle(b):
            a = o8 + W2 * b
            scan(T.mo[:, a:a + W2], T.ad[:, W2 * b:W2 * (b + 1)], T.pq[:, a:a + W2], 0.0, A.min, A.max,
                 [("ad", b), "ad0"] + [("pq", t, b, e, i) for e in range(2) for i in range(2)], [("mo", t, b)])

        regained = {}

        def regain(b, c0):
            if t + 1 == R and c0: return
            a, l = o8 + W2 * b, 32 * t + 16
            acp(T.mc2[:, C * b + c0:C * b + C], T.mo[:, a:a + W2].indirect(T.bl[:, l + c0 // 16:l + C // 16]), [("mo", t, b), ("bl", t, 0)], [("mc2", b)])
            regained[b] = c0

        def add(b, c0, c1, parts):
            a, l = o8 + W2 * b, 32 * t + 16
            if c0 >= regained.get(b, C):
                tt(xcol(t + 1, b, c0, c1), T.mc2[:, C * b + c0:C * b + c1], yw(b, c0, c1), A.add, [("mc2", b), ("yh", t, b)], [("xs", t + 1, b, c) for c in parts])
                return
            tt(xcol(t + 1, b, c0, c1), T.mo[:, a:a + W2].indirect(T.bl[:, l + c0 // 16:l + c1 // 16]), yw(b, c0, c1), A.add,
               [("mo", t, b), ("yh", t, b), ("bl", t, 0)], [("xs", t + 1, b, c) for c in parts])

        whole = t + 1 == R
        ca, u, x0 = OPT["ca"], t + 1, XP + o4
        head = lambda b: add(b, 0, C, (0, 1)) if whole or ca == C else add(b, 0, ca, (0,))
        steps = {"o": order, "f": fetch, "b": bring, "m": middle, "h": head, "g": lambda b: regain(b, ca), "G": lambda b: regain(b, 0)}
        for s in OPT["back"].split(): steps[s[0]](int(s[1]))
        if whole or ca == C:
            qz(*qx(u), T.xs[:, x0:x0 + 4 * C], xkeys(u), [("qx", u)])
            if not whole:
                products(u, C)
                d = direction(u)
                steps = {"d": lambda i: d[i](), "s": lambda i: sign(u, (0, 1), 1, 0, C, 0), "w": lambda b: vmul(u, b, (0, 1), 2 + b, 0, C, 0)}
                for s in OPT["seq"].split(): steps[s[0]](int(s[1]))
        else:
            for b in range(OPT["afill"]): add(b, ca, C, (1,))
            pa = 128 - ca
            qz(*qx(u, 128), T.xs[:, x0 + 4 * ca - 512:x0 + 4 * ca], xkeys(u, (0,)) + (xkeys(t, (1,)) + ["pad"] if pa else []), [("qx", u)])
            nb = C if OPT["ball"] else 128
            products(u, 128, not OPT["ball"])
            d = direction(u, pa)
            bc, bs = T.dc[:, C * t:C * t + nb], T.ds[:, C * t:C * t + nb]
            banks = (2, 3, 4, 5) if OPT["ball"] else (7, 1, 0, 2)
            cb = 0 if OPT["ball"] else ca
            pb, kb = cb - (C - nb), ((0, 1) if OPT["ball"] else (1,))

            def rest():
                qz(bc, bs, T.xs[:, x0 + 4 * (C - nb):x0 + 4 * C], xkeys(u), [("qb", u)])
                mm(ps(6)[:, 0:nb], T.upc[:, 128:256], T.ups[:, 128:256], bc, bs, [("qb", u), "upc1", "ups1"], [("ps", 6)])
                for b in range(4 if OPT["ball"] else 3): mm(ps(banks[b])[:, 0:nb], *eb(b), bc, bs, [("qb", u), ("e", b)], [("ps", banks[b])])
                sign(u, kb, 6, cb, C, pb)

            def first(b):
                vmul(u, b, (0,), 2 + b, 0, ca, pa)
                if b == 0: mm(ps(2)[:, 0:128], *eb(3), bc, bs, [("qb", u), ("e", 3)], [("ps", 2)])

            steps = {"a": lambda b: add(b, ca, C, (1,)), "d": lambda i: d[i](), "q": lambda i: rest(), "s": lambda i: sign(u, (0,), 1, 0, ca, pa),
                     "v": first, "w": lambda b: vmul(u, b, kb, banks[b], cb, C, pb)}
            for s in OPT["seq"].split(): steps[s[0]](int(s[1]))

    xc, xsc = qx(R)
    kq = [("qx", R)]
    mm(ps(0)[:, 0:C], T.vc[:], T.vs[:], xc, xsc, kq + ["vq"], [("ps", 0)])
    store("S", T.oc[:, :], xc.bitcast(dt.uint8), kq)
    c0 = C * (R - 1)
    for i in range(4):
        store("ASSS"[i], T.osc[4 * i:4 * i + 4, :], T.qs[32 * i:32 * i + 4, c0:c0 + C], kq)
    cp(T.yo[:], ps(0)[:, 0:C], [("ps", 0)], ["yo"])
    store("A", T.y[:, :], T.yo[:], ["yo"])
    emit(ops, queues, T, [("sent", sent[0]), ("st", stores[0])], landing)
